import numpy as np
import ml_dtypes


def mxq(x, axis, fmt="e4m3"):
    dtype, down = {"e4m3": (ml_dtypes.float8_e4m3fn, 7), "e5m2": (ml_dtypes.float8_e5m2, 14)}[fmt]
    v = np.moveaxis(np.asarray(x, np.float32).astype(ml_dtypes.bfloat16).astype(np.float64), axis, -1)
    blocks = v.reshape(v.shape[:-1] + (-1, 32))
    amax = np.abs(blocks).max(-1, keepdims=True)
    byte = np.maximum(np.where(amax > 0, np.frexp(amax)[1] - 1 + 127, 0) - down, 1)
    scale = np.exp2(byte - 127.0)
    codes = (blocks / scale).astype(np.float32).astype(dtype).astype(np.float64)
    return np.moveaxis((codes * scale).reshape(v.shape), -1, axis)


WIDE = False


def mx_kscale(k):
    if not WIDE:
        return np.ones(k)
    levels = np.array([10, -10, 5, -5, 0])
    if k % 512:
        return np.exp2(np.random.permutation(np.resize(levels, k // 32))).repeat(32)
    a = np.empty((k // 512, 16))
    for p in range(k // 512):
        a[p, :8] = np.random.permutation(np.resize(levels, 8))
        for g in range(8):
            far = levels[np.abs(levels - a[p, g]) >= 10]
            a[p, g + 8] = far[np.random.randint(len(far))]
    return np.exp2(a.ravel()).repeat(32)


BF16 = ml_dtypes.bfloat16


def bf(x):
    return np.asarray(x, np.float32).astype(BF16)


def f64(x):
    return np.asarray(x).astype(np.float64)

def planes(Y):
    n, m = Y.shape
    b = f64(bf(Y)).reshape(n // 32, 32, m)
    amax = np.abs(b).max(1)
    byte = np.clip(np.where(amax > 0, np.frexp(amax)[1] - 1 + 127 - 7, 1), 1, 254)
    codes = (b * np.exp2(127.0 - byte)[:, None, :]).reshape(n, m).astype(np.float32).astype(ml_dtypes.float8_e4m3fn).view(np.uint8)
    words = codes.reshape(n // 512, 128, 4, m).transpose(0, 1, 3, 2)
    return np.ascontiguousarray(words), np.ascontiguousarray(byte.astype(np.uint8).reshape(n // 512, 16, m))


N, D, M = 1024, 1024, 512


def sigmoid(v):
    return 1.0 / (1.0 + np.exp(-v))


def setup_inputs():
    p = mx_kscale(D)
    t = mx_kscale(N)
    sgn = np.where(np.random.standard_normal(D) > 0.0, 1.0, -1.0)
    return {
        "x": bf(np.random.standard_normal((N, D))),
        "s": bf(sgn * (1.0 + 0.2 * np.random.standard_normal(D)) * p),
        "w": bf(np.random.standard_normal((D, M)) * (2.0 / np.sqrt(D)) / p[:, None]),
        "y": bf(np.random.uniform(0.0, 1.0, (N, M))),
        "a": bf((1.0 + 0.2 * np.random.standard_normal(N)) * t),
        "b": bf((1.0 + 0.2 * np.random.standard_normal(N)) / t),
        "lam": bf(0.5 * np.random.standard_normal((D, M)) - 0.5),
    }


def loss_gradient(x, delta, a, b):
    xa = x * a[:, None]
    db = delta * b[:, None]
    return (mxq(xa, 0, "e4m3").T @ mxq(db, 0, "e4m3")) / np.sqrt(x.shape[0])


def core(x, s, w, y, a, b, lam):
    x, s, w, y, a, b, lam = f64(x), f64(s), f64(w), f64(y), f64(a), f64(b), f64(lam)
    z = mxq(x * s[None, :], 1, "e4m3") @ mxq(w, 0, "e4m3")
    u = s[:, None] * w

    delta = sigmoid(z) - y

    grad = loss_gradient(x, delta, a, b)

    lam1 = lam + 2.0 * np.exp(lam) * np.sign(u) * grad

    return lam1 - np.mean(lam1) - 1.0


def reference(x, s, w, y, a, b, lam):
    R_out = core(x, s, w, y, a, b, lam)
    words, scales = planes(R_out.T)
    return R_out, words, scales

@@ -1,0 +1,390 @@
+from contextlib import ExitStack
+
+import concourse.mybir as mybir
+from concourse.masks import make_identity
+
+F32 = mybir.dt.float32
+BF16 = mybir.dt.bfloat16
+U32 = mybir.dt.uint32
+I32 = mybir.dt.int32
+U8 = mybir.dt.uint8
+FP8X4 = mybir.dt.float8_e4m3fn_x4
+ALU = mybir.AluOpType
+ACT = mybir.ActivationFunctionType
+
+N, D, M = 1024, 1024, 512
+P = 128
+FLOPS = 2 * 2 * N * D * M
+
+
+def tile_regularizationlearningnetworkcoefficient_x1_kernel(
+    tc, x, s, w, y, a, b, lam, out_0, out_1, out_2
+):
+    nc = tc.nc
+    with ExitStack() as ctx:
+        keep = ctx.enter_context(tc.tile_pool(name="keep", bufs=1))
+        ps_tp = ctx.enter_context(tc.psum_pool(name="ps_tp", bufs=2))
+        ps_bk = ctx.enter_context(tc.psum_pool(name="ps_bk", bufs=5))
+        ps_sm = ctx.enter_context(tc.psum_pool(name="ps_sm", bufs=1))
+
+        roll = ctx.enter_context(tc.tile_pool(name="roll", bufs=4))
+
+        def T(name, shape, dt):
+            return keep.tile(shape, dt, name=name, align_bytes=64)
+
+        s8 = T("s8", [P, 2, 4], BF16)
+        a8 = T("a8", [P, 2, 4], BF16)
+        b8 = T("b8", [P, 2, 4], BF16)
+        sf = T("sf", [P, 8], F32)
+        af = T("af", [P, 8], F32)
+        bfl = T("bfl", [P, 8], F32)
+        bh = T("bh", [P, 8], F32)
+        idf = T("idf", [P, P], F32)
+        idb = T("idb", [P, P], BF16)
+        negs = T("negs", [P, P], F32)
+        one = T("one", [P, 1], BF16)
+        diag = T("diag", [P, 8, P], BF16)
+        xt = [T("xt%d" % i, [P, D], BF16) for i in range(8)]
+        wt = [T("wt%d" % g, [P, 4, M], BF16) for g in range(2)]
+        yt = [T("yt%d" % g, [P, 4, M], BF16) for g in range(2)]
+        lt = [T("lt%d" % g, [P, 4, M], BF16) for g in range(2)]
+        wg = [T("wg%d" % g, [P, M, 4], BF16) for g in range(2)]
+        wc = [T("wc%d" % g, [P, M], U32) for g in range(2)]
+        ws = [T("ws%d" % g, [P, M], U8) for g in range(2)]
+        xsc = [T("xsc%d" % i, [P, 2 * P], U32) for i in range(8)]
+        xss = [T("xss%d" % i, [P, 2 * P], U8) for i in range(8)]
+        yb = [T("yb%d" % i, [P, M], F32) for i in range(8)]
+        dbr = [T("dbr%d" % g, [P, 4, M], BF16) for g in range(2)]
+        dbg = [T("dbg%d" % g, [P, M, 4], BF16) for g in range(2)]
+        dbc = [T("dbc%d" % g, [P, M], U32) for g in range(2)]
+        dbs = [T("dbs%d" % g, [P, M], U8) for g in range(2)]
+        xr = T("xr", [P, 4, 512], BF16)
+        xag = [T("xag%d" % g, [P, 2, 4, P, 4], BF16) for g in range(2)]
+        xac = [T("xac%d" % g, [P, D], U32) for g in range(2)]
+        xas = [T("xas%d" % g, [P, D], U8) for g in range(2)]
+        sg = [T("sg%d" % i, [P, M], BF16) for i in range(8)]
+        cc = [T("cc%d" % i, [P, M], F32) for i in range(8)]
+        tt = [T("tt%d" % i, [P, M], F32) for i in range(8)]
+        stats = T("stats", [P, 8], F32)
+        lamst = T("lamst", [P, 1], F32)
+        sh = T("sh", [P, 1], F32)
+        o32 = cc
+        o16 = [T("o16_%d" % i, [P, 2, P, 2], BF16) for i in range(8)]
+        pg = [T("pg%d" % g, [P, 512, 4], BF16) for g in range(2)]
+        pc = [T("pc%d" % g, [P, 512], U32) for g in range(2)]
+        psc = [T("psc%d" % g, [P, 512], U8) for g in range(2)]
+
+        ctx.enter_context(tc.manual_schedule())
+        xsg, th, ex = {}, {}, {}
+
+        def vec(v):
+            return v.rearrange("(g p t) -> p g t", g=2, t=4)
+
+        nc.scalar.dma_start(out=s8[:], in_=vec(s))
+        nc.scalar.dma_start(out=a8[:], in_=vec(a))
+        nc.scalar.dma_start(out=b8[:], in_=vec(b))
+        x4 = x.rearrange("(g p t) d -> g t p d", g=2, t=4)
+        w4 = w.rearrange("(g p t) m -> g p t m", g=2, t=4)
+        y4 = y.rearrange("(g p t) m -> g p t m", g=2, t=4)
+        l4 = lam.rearrange("(g p t) m -> g p t m", g=2, t=4)
+
+        def ldx(i):
+            nc.sync.dma_start(out=xt[i][:], in_=x4[i // 4, i % 4])
+
+        ldx(0)
+        nc.sync.dma_start(out=wt[0][:], in_=w4[0])
+        nc.sync.dma_start(out=wt[1][:], in_=w4[1])
+        ldx(1)
+        ldx(2)
+        ldx(3)
+        nc.sync.dma_start(out=yt[0][:], in_=y4[0])
+        for i in range(4, 8):
+            ldx(i)
+        nc.sync.dma_start(out=yt[1][:], in_=y4[1])
+        nc.sync.dma_start(out=lt[0][:], in_=l4[0])
+        nc.sync.dma_start(out=lt[1][:], in_=l4[1])
+
+        make_identity(nc, idf[:])
+        nc.gpsimd.tensor_copy(out=idb[:], in_=idf[:])
+        nc.gpsimd.memset(negs[:], -1.0 / (D * M))
+        nc.gpsimd.memset(one[:], 1.0)
+        fl = lambda t: t[:].rearrange("p g t -> p (g t)")
+        nc.gpsimd.tensor_copy(out=sf[:], in_=fl(s8))
+        nc.gpsimd.tensor_copy(out=af[:], in_=fl(a8))
+        nc.gpsimd.tensor_copy(out=bfl[:], in_=fl(b8))
+        nc.gpsimd.tensor_scalar(out=bh[:], in0=fl(b8), scalar1=0.5, scalar2=0.0, op0=ALU.mult, op1=ALU.add)
+        for k in range(8):
+            nc.gpsimd.tensor_scalar(
+                out=diag[:, k, :], in0=idb[:], scalar1=af[:, k : k + 1], scalar2=1.0, op0=ALU.mult, op1=ALU.mult
+            )
+
+        tp = {}
+        bank = {}
+
+        def X(i):
+            t_ = ps_tp.tile([P, 2, 2, P], F32, name="tp")
+            tp[i] = t_
+            words = xt[i][:].bitcast(F32)
+            for gd in range(2):
+                for u in range(2):
+                    nc.tensor.transpose(t_[:, gd, u, :], words[:, 256 * gd + u : 256 * (gd + 1) : 2], idf[:])
+
+        def XS(i):
+            xsg[i] = roll.tile([P, 2, P, 4], BF16, name="xsg", align_bytes=64)
+            for gd in range(2):
+                src = tp[i][:, gd].bitcast(BF16).rearrange("p u (n e) -> p n u e", e=2)
+                fac = s8[:, gd, :].unsqueeze(1).to_broadcast([P, P, 4]).rearrange("p n (u e) -> p n u e", e=2)
+                nc.vector.tensor_tensor(
+                    out=xsg[i][:, gd].rearrange("p n (u e) -> p n u e", e=2), in0=src, in1=fac, op=ALU.mult
+                )
+
+        def XQ(i):
+            nc.vector.quantize_mx(
+                out=xsc[i][:].bitcast(FP8X4), scales=xss[i][:], in_=xsg[i][:].rearrange("p g n t -> p (g n t)")
+            )
+
+        def WI(g):
+            nc.vector.tensor_copy(out=wg[g][:, 0:256, :], in_=wt[g][:, :, 0:256].rearrange("p t m -> p m t"))
+            nc.scalar.copy(out=wg[g][:, 256:512, :], in_=wt[g][:, :, 256:512].rearrange("p t m -> p m t"))
+
+        def WQ(g):
+            nc.vector.quantize_mx(
+                out=wc[g][:].bitcast(FP8X4), scales=ws[g][:], in_=wg[g][:].rearrange("p m t -> p (m t)")
+            )
+
+        def Z(i):
+            z_ = ps_bk.tile([P, M], F32, name="bk")
+            bank["z", i] = z_
+            for gd in range(2):
+                c = slice(gd * P, gd * P + P)
+                nc.tensor.matmul_mx(
+                    out=z_[:], lhsT=xsc[i][:, c].bitcast(FP8X4), lhsT_scale=xss[i][:, c],
+                    rhs=wc[gd][:].bitcast(FP8X4), rhs_scale=ws[gd][:], start=(gd == 0), stop=(gd == 1),
+                )
+
+        def TH(i):
+            th[i] = roll.tile([P, M], F32, name="th", align_bytes=64)
+            nc.scalar.activation(out=th[i][:], in_=bank["z", i][:], func=ACT.Tanh, scale=0.5)
+
+        def YB(i):
+            nc.gpsimd.tensor_scalar(
+                out=yb[i][:], in0=yt[i // 4][:, i % 4, :], scalar1=-0.5, scalar2=bfl[:, i : i + 1],
+                op0=ALU.add, op1=ALU.mult,
+            )
+
+        def DB(i):
+            nc.vector.scalar_tensor_tensor(
+                out=dbr[i // 4][:, i % 4, :], in0=th[i][:], scalar=bh[:, i : i + 1], in1=yb[i][:],
+                op0=ALU.mult, op1=ALU.subtract,
+            )
+
+        def DG(g):
+            nc.vector.tensor_copy(out=dbg[g][:, 0:256, :], in_=dbr[g][:, :, 0:256].rearrange("p t m -> p m t"))
+            nc.scalar.copy(out=dbg[g][:, 256:512, :], in_=dbr[g][:, :, 256:512].rearrange("p t m -> p m t"))
+
+        def DQ(g):
+            nc.vector.quantize_mx(
+                out=dbc[g][:].bitcast(FP8X4), scales=dbs[g][:], in_=dbg[g][:].rearrange("p m t -> p (m t)")
+            )
+
+        def XR():
+            for t in range(4):
+                nc.vector.tensor_scalar(
+                    out=xr[:, t, :], in0=xt[t][:, 0:512], scalar1=af[:, t : t + 1], scalar2=None, op0=ALU.mult
+                )
+
+        def XAV():
+            nc.vector.tensor_copy(out=xag[0][:, 0], in_=xr[:].rearrange("p t (q j) -> p j q t", j=4))
+
+        def XA(g, dc):
+            k_ = ps_bk.tile([P, 4, P], F32, name="bk")
+            for t in range(4):
+                nc.tensor.matmul(
+                    out=k_[:, t, :], lhsT=diag[:, 4 * g + t, :], rhs=xt[4 * g + t][:, P * dc : P * dc + P],
+                    start=True, stop=True,
+                )
+            r = 32 * (dc % 4)
+            nc.scalar.copy(
+                out=xag[g][:, dc // 4, :, r : r + 32, :], in_=k_[:].rearrange("p t (q j) -> p j q t", j=4)
+            )
+
+        def XAQ(g, gd):
+            c = slice(512 * gd, 512 * gd + 512)
+            nc.vector.quantize_mx(
+                out=xac[g][:, c].bitcast(FP8X4), scales=xas[g][:, c],
+                in_=xag[g][:, gd].rearrange("p j q t -> p (j q t)"),
+            )
+
+        def SG(i):
+            nc.scalar.activation(out=sg[i][:], in_=wt[i // 4][:, i % 4, :], func=ACT.Sign, scale=sf[:, i : i + 1])
+
+        def EX(i):
+            ex[i] = roll.tile([P, M], F32, name="ex", align_bytes=64)
+            nc.scalar.activation(out=ex[i][:], in_=lt[i // 4][:, i % 4, :], func=ACT.Exp)
+
+        def C(i):
+            nc.vector.tensor_tensor(out=cc[i][:], in0=ex[i][:], in1=sg[i][:], op=ALU.mult)
+
+        def GR(i):
+            g_ = ps_bk.tile([P, M], F32, name="bk")
+            bank["g", i] = g_
+            c = slice(P * i, P * i + P)
+            for g in range(2):
+                nc.tensor.matmul_mx(
+                    out=g_[:], lhsT=xac[g][:, c].bitcast(FP8X4), lhsT_scale=xas[g][:, c],
+                    rhs=dbc[g][:].bitcast(FP8X4), rhs_scale=dbs[g][:], start=(g == 0), stop=(g == 1),
+                )
+
+        def NN(i):
+            nc.vector.scalar_tensor_tensor(
+                out=tt[i][:], in0=bank["g", i][:], scalar=1.0 / 16.0, in1=cc[i][:], op0=ALU.mult, op1=ALU.mult,
+                accum_out=stats[:, i : i + 1],
+            )
+
+        for i in range(8):
+            YB(i)
+        X(0)
+        WI(0)
+        XS(0)
+        WQ(0)
+        WI(1)
+        XQ(0)
+        X(1)
+        WQ(1)
+        for i in range(1, 9):
+            if i < 8:
+                XS(i)
+                if i < 7:
+                    X(i + 1)
+            Z(i - 1)
+            TH(i - 1)
+            if i >= 2:
+                DB(i - 2)
+            if i < 8:
+                XQ(i)
+            if i <= 3:
+                SG(2 * i - 2)
+                SG(2 * i - 1)
+            if i == 4:
+                XR()
+            if i in (4, 5, 6, 7):
+                XA(0, i)
+            if i == 5:
+                DG(0)
+                SG(6)
+            if i == 6:
+                XAV()
+                DQ(0)
+                SG(7)
+            if i == 7:
+                XAQ(0, 0)
+        for dc in range(4):
+            XA(1, dc)
+        EX(0)
+        DB(7)
+        XAQ(1, 0)
+        DG(1)
+        EX(1)
+        C(0)
+        for dc in range(4, 8):
+            XA(1, dc)
+        for i in range(2, 8):
+            EX(i)
+        sm = ps_sm.tile([P, 2], F32, name="sm")
+        for k in range(32):
+            nc.tensor.matmul(
+                out=sm[:, 0:1], lhsT=lt[k // 16][:, (k // 4) % 4, P * (k % 4) : P * (k % 4) + P], rhs=one[:],
+                start=(k == 0), stop=(k == 31),
+            )
+        DQ(1)
+        C(1)
+        nc.vector.tensor_copy(out=lamst[:], in_=sm[:, 0:1])
+
+        def SUM(i):
+            src = lamst[:] if i < 0 else stats[:, i : i + 1]
+            nc.tensor.matmul(out=sm[:, 1:2], lhsT=negs[:], rhs=src, start=(i < 0), stop=(i == 7))
+
+        SUM(-1)
+        GR(0)
+        GR(1)
+        XAQ(0, 1)
+        for i in range(8):
+            if i + 2 < 8:
+                GR(i + 2)
+            NN(i)
+            if i == 1:
+                XAQ(1, 1)
+            if i + 2 < 8:
+                C(i + 2)
+            if i < 4:
+                nc.gpsimd.tensor_tensor(
+                    out=tt[i][:], in0=tt[i][:], in1=lt[0][:, i, :], op=ALU.add
+                )
+            if i > 0:
+                SUM(i - 1)
+        SUM(7)
+        nc.vector.tensor_scalar(out=sh[:], in0=sm[:, 1:2], scalar1=-1.0, scalar2=None, op0=ALU.add)
+
+        o4 = out_0.rearrange("(g p t) m -> g t p m", g=2, t=4)
+        o1 = out_1.rearrange("g p m t -> (g p) (m t)").bitcast(I32)
+        o2 = out_2.rearrange("g q m -> (g q) m").bitcast(I32)
+
+        def perm(t_):
+            return t_[:].rearrange("p (q u e) -> p u q e", u=2, e=2)
+
+        def O(i):
+            if i < 4:
+                nc.scalar.activation(out=o32[i][:], in_=tt[i][:], func=ACT.Identity, bias=sh[:])
+                nc.vector.tensor_scalar(out=o16[i][:], in0=perm(tt[i]), scalar1=sh[:], scalar2=None, op0=ALU.add)
+            else:
+                nc.vector.scalar_tensor_tensor(
+                    out=o32[i][:], in0=tt[i][:], scalar=sh[:], in1=lt[1][:, i - 4, :], op0=ALU.add, op1=ALU.add
+                )
+            nc.sync.dma_start(out=o4[i // 4, i % 4], in_=o32[i][:])
+
+        pt = {}
+
+        def PT(gd, jh):
+            p_ = ps_tp.tile([P, 2, 2, P], F32, name="tp")
+            pt[gd, jh] = p_
+            for jj in range(2):
+                words = o16[4 * gd + 2 * jh + jj][:].rearrange("p u q e -> p (u q e)").bitcast(F32)
+                for u in range(2):
+                    nc.tensor.transpose(p_[:, jj, u, :], words[:, P * u : P * u + P], idf[:])
+
+        def PC(gd, jh, eng):
+            dst = pg[gd][:].rearrange("p m t -> p (m t)").bitcast(F32).rearrange("p (q j u) -> p q j u", j=4, u=2)
+            eng(out=dst[:, :, 2 * jh : 2 * jh + 2, :], in_=pt[gd, jh][:].rearrange("p j u q -> p q j u"))
+
+        def PQ(gd):
+            nc.vector.quantize_mx(
+                out=pc[gd][:].bitcast(FP8X4), scales=psc[gd][:], in_=pg[gd][:].rearrange("p m t -> p (m t)")
+            )
+            nc.sync.dma_start(out=o1[:, 512 * gd : 512 * gd + 512], in_=pc[gd][:].bitcast(I32))
+            for q in range(4):
+                nc.sync.dma_start(
+                    out=o2[4 * q : 4 * q + 4, 128 * gd : 128 * gd + 128], in_=psc[gd][32 * q : 32 * q + 4, :].bitcast(I32)
+                )
+
+        O(0)
+        O(1)
+        PT(0, 0)
+        O(2)
+        O(3)
+        PT(0, 1)
+        O(4)
+        PC(0, 0, nc.scalar.copy)
+        O(5)
+        for i in (4, 5):
+            nc.vector.tensor_copy(out=o16[i][:], in_=perm(o32[i]))
+        PT(1, 0)
+        PC(0, 1, nc.scalar.copy)
+        O(6)
+        O(7)
+        PQ(0)
+        nc.vector.tensor_copy(out=o16[6][:], in_=perm(o32[6]))
+        nc.vector.tensor_copy(out=o16[7][:], in_=perm(o32[7]))
+        PT(1, 1)
+        PC(1, 0, nc.scalar.copy)
+        PC(1, 1, nc.vector.tensor_copy)
+        PQ(1)

@@ -14,6 +14,7 @@ ACT = mybir.ActivationFunctionType
 
 N, D, M = 1024, 1024, 512
 P = 128
+BIG = 2.0**100
 FLOPS = 2 * 2 * N * D * M
 
 
@@ -39,6 +40,7 @@ def tile_regularizationlearningnetworkcoefficient_x1_kernel(
         af = T("af", [P, 8], F32)
         bfl = T("bfl", [P, 8], F32)
         bh = T("bh", [P, 8], F32)
+        nbh = T("nbh", [P, 8], F32)
         idf = T("idf", [P, P], F32)
         idb = T("idb", [P, P], BF16)
         negs = T("negs", [P, P], F32)
@@ -81,8 +83,10 @@ def tile_regularizationlearningnetworkcoefficient_x1_kernel(
             return v.rearrange("(g p t) -> p g t", g=2, t=4)
 
         nc.scalar.dma_start(out=s8[:], in_=vec(s))
-        nc.scalar.dma_start(out=a8[:], in_=vec(a))
+        nc.gpsimd.dma_start(out=a8[:], in_=vec(a))
         nc.scalar.dma_start(out=b8[:], in_=vec(b))
+        nc.vector.memset(sh[:], 0.0)
+        nc.scalar.activation(out=sh[:], in_=sh[:], func=ACT.Tanh)
         x4 = x.rearrange("(g p t) d -> g t p d", g=2, t=4)
         w4 = w.rearrange("(g p t) m -> g p t m", g=2, t=4)
         y4 = y.rearrange("(g p t) m -> g p t m", g=2, t=4)
@@ -91,14 +95,12 @@ def tile_regularizationlearningnetworkcoefficient_x1_kernel(
         def ldx(i):
             nc.sync.dma_start(out=xt[i][:], in_=x4[i // 4, i % 4])
 
-        ldx(0)
         nc.sync.dma_start(out=wt[0][:], in_=w4[0])
+        ldx(0)
         nc.sync.dma_start(out=wt[1][:], in_=w4[1])
         ldx(1)
-        ldx(2)
-        ldx(3)
         nc.sync.dma_start(out=yt[0][:], in_=y4[0])
-        for i in range(4, 8):
+        for i in range(2, 8):
             ldx(i)
         nc.sync.dma_start(out=yt[1][:], in_=y4[1])
         nc.sync.dma_start(out=lt[0][:], in_=l4[0])
@@ -109,14 +111,11 @@ def tile_regularizationlearningnetworkcoefficient_x1_kernel(
         nc.gpsimd.memset(negs[:], -1.0 / (D * M))
         nc.gpsimd.memset(one[:], 1.0)
         fl = lambda t: t[:].rearrange("p g t -> p (g t)")
-        nc.gpsimd.tensor_copy(out=sf[:], in_=fl(s8))
+        nc.gpsimd.tensor_scalar(out=sf[:], in0=fl(s8), scalar1=BIG, scalar2=0.0, op0=ALU.mult, op1=ALU.add)
         nc.gpsimd.tensor_copy(out=af[:], in_=fl(a8))
         nc.gpsimd.tensor_copy(out=bfl[:], in_=fl(b8))
         nc.gpsimd.tensor_scalar(out=bh[:], in0=fl(b8), scalar1=0.5, scalar2=0.0, op0=ALU.mult, op1=ALU.add)
-        for k in range(8):
-            nc.gpsimd.tensor_scalar(
-                out=diag[:, k, :], in0=idb[:], scalar1=af[:, k : k + 1], scalar2=1.0, op0=ALU.mult, op1=ALU.mult
-            )
+        nc.gpsimd.tensor_scalar(out=nbh[:], in0=fl(b8), scalar1=-0.5, scalar2=0.0, op0=ALU.mult, op1=ALU.add)
 
         tp = {}
         bank = {}
@@ -167,10 +166,14 @@ def tile_regularizationlearningnetworkcoefficient_x1_kernel(
             nc.scalar.activation(out=th[i][:], in_=bank["z", i][:], func=ACT.Tanh, scale=0.5)
 
         def YB(i):
-            nc.gpsimd.tensor_scalar(
-                out=yb[i][:], in0=yt[i // 4][:, i % 4, :], scalar1=-0.5, scalar2=bfl[:, i : i + 1],
-                op0=ALU.add, op1=ALU.mult,
+            nc.scalar.activation(
+                out=yb[i][:], in_=yt[i // 4][:, i % 4, :], func=ACT.Identity, scale=bfl[:, i : i + 1],
+                bias=nbh[:, i : i + 1],
             )
+
+        def DI(g):
+            for k in range(4 * g, 4 * g + 4):
+                nc.scalar.activation(out=diag[:, k, :], in_=idb[:], func=ACT.Copy, scale=af[:, k : k + 1])
 
         def DB(i):
             nc.vector.scalar_tensor_tensor(
@@ -216,14 +219,19 @@ def tile_regularizationlearningnetworkcoefficient_x1_kernel(
             )
 
         def SG(i):
-            nc.scalar.activation(out=sg[i][:], in_=wt[i // 4][:, i % 4, :], func=ACT.Sign, scale=sf[:, i : i + 1])
+            nc.vector.tensor_scalar(
+                out=sg[i][:], in0=wt[i // 4][:, i % 4, :], scalar1=sf[:, i : i + 1], scalar2=1.0,
+                op0=ALU.mult, op1=ALU.min,
+            )
 
         def EX(i):
             ex[i] = roll.tile([P, M], F32, name="ex", align_bytes=64)
             nc.scalar.activation(out=ex[i][:], in_=lt[i // 4][:, i % 4, :], func=ACT.Exp)
 
         def C(i):
-            nc.vector.tensor_tensor(out=cc[i][:], in0=ex[i][:], in1=sg[i][:], op=ALU.mult)
+            nc.vector.scalar_tensor_tensor(
+                out=cc[i][:], in0=sg[i][:], scalar=-1.0, in1=ex[i][:], op0=ALU.max, op1=ALU.mult
+            )
 
         def GR(i):
             g_ = ps_bk.tile([P, M], F32, name="bk")
@@ -241,88 +249,103 @@ def tile_regularizationlearningnetworkcoefficient_x1_kernel(
                 accum_out=stats[:, i : i + 1],
             )
 
-        for i in range(8):
-            YB(i)
+        others = [lambda i=i: YB(i) for i in range(2)]
+        others += [lambda: XA(0, 4), lambda: YB(2), lambda: XA(0, 5), lambda: YB(3)]
+        others += [lambda: XA(0, 6), lambda: YB(4), lambda: XA(0, 7), lambda: YB(5)]
+        others += [lambda: XA(1, 0), lambda: YB(6), lambda: XA(1, 1), lambda: YB(7)]
+        others += [lambda: XA(1, 2), lambda: EX(0), lambda: XA(1, 3)]
+        others += [lambda: EX(1), lambda: XA(1, 4), lambda: EX(2), lambda: XA(1, 5)]
+        others += [lambda: EX(3), lambda: XA(1, 6), lambda: EX(4), lambda: XA(1, 7)]
+        others += [lambda i=i: EX(i) for i in range(5, 8)]
+
+        def S(n):
+            for k in range(n):
+                if others:
+                    others.pop(0)()
+
         X(0)
+        X(1)
         WI(0)
         XS(0)
         WQ(0)
         WI(1)
         XQ(0)
-        X(1)
+        XS(1)
         WQ(1)
-        for i in range(1, 9):
-            if i < 8:
+        DI(0)
+        S(1)
+        DI(1)
+        XQ(1)
+        X(2)
+        for k in range(4):
+            SG(k)
+        for i in range(1, 11):
+            if i <= 8:
+                Z(i - 1)
+            if 2 <= i < 8:
                 XS(i)
                 if i < 7:
                     X(i + 1)
-            Z(i - 1)
-            TH(i - 1)
-            if i >= 2:
-                DB(i - 2)
-            if i < 8:
+            if i <= 8:
+                TH(i - 1)
+            if i >= 3:
+                DB(i - 3)
+            if 2 <= i < 8:
                 XQ(i)
-            if i <= 3:
-                SG(2 * i - 2)
-                SG(2 * i - 1)
-            if i == 4:
+            if i <= 9:
+                S(2)
+            if i == 3:
                 XR()
-            if i in (4, 5, 6, 7):
-                XA(0, i)
-            if i == 5:
-                DG(0)
-                SG(6)
-            if i == 6:
+            if i == 4:
                 XAV()
-                DQ(0)
-                SG(7)
-            if i == 7:
+            if i == 5:
                 XAQ(0, 0)
-        for dc in range(4):
-            XA(1, dc)
-        EX(0)
-        DB(7)
-        XAQ(1, 0)
-        DG(1)
-        EX(1)
+            if i == 6:
+                DG(0)
+            if i == 7:
+                DQ(0)
+            if i == 8:
+                for k in range(4, 8):
+                    SG(k)
+            if i == 9:
+                XAQ(0, 1)
         C(0)
-        for dc in range(4, 8):
-            XA(1, dc)
-        for i in range(2, 8):
-            EX(i)
+        DG(1)
+        S(2)
+        S(19)
+        C(1)
+        DQ(1)
+        C(2)
+        XAQ(1, 0)
+        C(3)
         sm = ps_sm.tile([P, 2], F32, name="sm")
         for k in range(32):
             nc.tensor.matmul(
                 out=sm[:, 0:1], lhsT=lt[k // 16][:, (k // 4) % 4, P * (k % 4) : P * (k % 4) + P], rhs=one[:],
                 start=(k == 0), stop=(k == 31),
             )
-        DQ(1)
-        C(1)
-        nc.vector.tensor_copy(out=lamst[:], in_=sm[:, 0:1])
 
         def SUM(i):
             src = lamst[:] if i < 0 else stats[:, i : i + 1]
             nc.tensor.matmul(out=sm[:, 1:2], lhsT=negs[:], rhs=src, start=(i < 0), stop=(i == 7))
 
-        SUM(-1)
-        GR(0)
-        GR(1)
-        XAQ(0, 1)
+        C(4)
+        XAQ(1, 1)
+        nc.vector.tensor_copy(out=lamst[:], in_=sm[:, 0:1])
+        for i in range(4):
+            GR(i)
+        for i in range(5, 8):
+            C(i)
         for i in range(8):
-            if i + 2 < 8:
-                GR(i + 2)
             NN(i)
-            if i == 1:
-                XAQ(1, 1)
-            if i + 2 < 8:
-                C(i + 2)
+            if i + 4 < 8:
+                GR(i + 4)
             if i < 4:
                 nc.gpsimd.tensor_tensor(
                     out=tt[i][:], in0=tt[i][:], in1=lt[0][:, i, :], op=ALU.add
                 )
-            if i > 0:
-                SUM(i - 1)
-        SUM(7)
+        for i in range(-1, 8):
+            SUM(i)
         nc.vector.tensor_scalar(out=sh[:], in0=sm[:, 1:2], scalar1=-1.0, scalar2=None, op0=ALU.add)
 
         o4 = out_0.rearrange("(g p t) m -> g t p m", g=2, t=4)

@@ -15,6 +15,8 @@ ACT = mybir.ActivationFunctionType
 N, D, M = 1024, 1024, 512
 P = 128
 BIG = 2.0**100
+OFF = 2
+PRE = (2, 7)
 FLOPS = 2 * 2 * N * D * M
 
 
@@ -68,7 +70,9 @@ def tile_regularizationlearningnetworkcoefficient_x1_kernel(
         cc = [T("cc%d" % i, [P, M], F32) for i in range(8)]
         tt = [T("tt%d" % i, [P, M], F32) for i in range(8)]
         stats = T("stats", [P, 8], F32)
-        lamst = T("lamst", [P, 1], F32)
+        st2 = T("st2", [P, OFF], F32)
+        gs = [T("gs%d" % i, [P, M], F32) for i in range(OFF)]
+        lamst = T("lamst", [P, 2], F32)
         sh = T("sh", [P, 1], F32)
         o32 = cc
         o16 = [T("o16_%d" % i, [P, 2, P, 2], BF16) for i in range(8)]
@@ -110,6 +114,7 @@ def tile_regularizationlearningnetworkcoefficient_x1_kernel(
         nc.gpsimd.tensor_copy(out=idb[:], in_=idf[:])
         nc.gpsimd.memset(negs[:], -1.0 / (D * M))
         nc.gpsimd.memset(one[:], 1.0)
+        nc.gpsimd.memset(lamst[:, 1:2], float(D * M // P))
         fl = lambda t: t[:].rearrange("p g t -> p (g t)")
         nc.gpsimd.tensor_scalar(out=sf[:], in0=fl(s8), scalar1=BIG, scalar2=0.0, op0=ALU.mult, op1=ALU.add)
         nc.gpsimd.tensor_copy(out=af[:], in_=fl(a8))
@@ -166,9 +171,9 @@ def tile_regularizationlearningnetworkcoefficient_x1_kernel(
             nc.scalar.activation(out=th[i][:], in_=bank["z", i][:], func=ACT.Tanh, scale=0.5)
 
         def YB(i):
-            nc.scalar.activation(
-                out=yb[i][:], in_=yt[i // 4][:, i % 4, :], func=ACT.Identity, scale=bfl[:, i : i + 1],
-                bias=nbh[:, i : i + 1],
+            nc.gpsimd.tensor_scalar(
+                out=yb[i][:], in0=yt[i // 4][:, i % 4, :], scalar1=-0.5, scalar2=bfl[:, i : i + 1],
+                op0=ALU.add, op1=ALU.mult,
             )
 
         def DI(g):
@@ -197,7 +202,11 @@ def tile_regularizationlearningnetworkcoefficient_x1_kernel(
                 )
 
         def XAV():
-            nc.vector.tensor_copy(out=xag[0][:, 0], in_=xr[:].rearrange("p t (q j) -> p j q t", j=4))
+            for eng, j0 in ((nc.vector.tensor_copy, 0), (nc.scalar.copy, 2)):
+                eng(
+                    out=xag[0][:, 0, j0 : j0 + 2],
+                    in_=xr[:].rearrange("p t (q j) -> p j q t", j=4)[:, j0 : j0 + 2],
+                )
 
         def XA(g, dc):
             k_ = ps_bk.tile([P, 4, P], F32, name="bk")
@@ -303,10 +312,10 @@ def tile_regularizationlearningnetworkcoefficient_x1_kernel(
             if i == 6:
                 DG(0)
             if i == 7:
-                DQ(0)
-            if i == 8:
                 for k in range(4, 8):
                     SG(k)
+            if i == 8:
+                DQ(0)
             if i == 9:
                 XAQ(0, 1)
         C(0)
@@ -326,27 +335,31 @@ def tile_regularizationlearningnetworkcoefficient_x1_kernel(
             )
 
         def SUM(i):
-            src = lamst[:] if i < 0 else stats[:, i : i + 1]
-            nc.tensor.matmul(out=sm[:, 1:2], lhsT=negs[:], rhs=src, start=(i < 0), stop=(i == 7))
+            src = (lamst[:, 0:1] if i == -1 else lamst[:, 1:2]) if i < 0 else (st2 if i < OFF else stats)[:, i : i + 1]
+            nc.tensor.matmul(out=sm[:, 1:2], lhsT=negs[:], rhs=src, start=(i == -2), stop=(i == 7))
 
         C(4)
         XAQ(1, 1)
-        nc.vector.tensor_copy(out=lamst[:], in_=sm[:, 0:1])
+        nc.vector.tensor_copy(out=lamst[:, 0:1], in_=sm[:, 0:1])
         for i in range(4):
             GR(i)
         for i in range(5, 8):
             C(i)
-        for i in range(8):
+        for i in range(OFF):
+            nc.scalar.activation(out=gs[i][:], in_=bank["g", i][:], func=ACT.Copy, scale=1.0 / 16.0)
+        for i in range(OFF):
+            nc.gpsimd.tensor_tensor(out=tt[i][:], in0=gs[i][:], in1=cc[i][:], op=ALU.mult)
+            nc.scalar.activation(out=gs[i][:], in_=tt[i][:], func=ACT.Identity, accum_out=st2[:, i : i + 1])
+        for i in range(OFF, 8):
             NN(i)
-            if i + 4 < 8:
-                GR(i + 4)
-            if i < 4:
-                nc.gpsimd.tensor_tensor(
-                    out=tt[i][:], in0=tt[i][:], in1=lt[0][:, i, :], op=ALU.add
+            if 4 <= i + 4 - OFF < 8:
+                GR(i + 4 - OFF)
+            if i in PRE:
+                (nc.vector if i == 7 else nc.gpsimd).tensor_tensor(
+                    out=tt[i][:], in0=tt[i][:], in1=lt[i // 4][:, i % 4, :], op=ALU.add
                 )
-        for i in range(-1, 8):
+        for i in (-2, -1, 2, 3, 0, 4, 5, 1, 6, 7):
             SUM(i)
-        nc.vector.tensor_scalar(out=sh[:], in0=sm[:, 1:2], scalar1=-1.0, scalar2=None, op0=ALU.add)
 
         o4 = out_0.rearrange("(g p t) m -> g t p m", g=2, t=4)
         o1 = out_1.rearrange("g p m t -> (g p) (m t)").bitcast(I32)
@@ -355,15 +368,22 @@ def tile_regularizationlearningnetworkcoefficient_x1_kernel(
         def perm(t_):
             return t_[:].rearrange("p (q u e) -> p u q e", u=2, e=2)
 
+        nc.vector.tensor_copy(out=sh[:], in_=sm[:, 1:2])
+
         def O(i):
-            if i < 4:
+            if i in PRE:
                 nc.scalar.activation(out=o32[i][:], in_=tt[i][:], func=ACT.Identity, bias=sh[:])
-                nc.vector.tensor_scalar(out=o16[i][:], in0=perm(tt[i]), scalar1=sh[:], scalar2=None, op0=ALU.add)
             else:
                 nc.vector.scalar_tensor_tensor(
-                    out=o32[i][:], in0=tt[i][:], scalar=sh[:], in1=lt[1][:, i - 4, :], op0=ALU.add, op1=ALU.add
+                    out=o32[i][:], in0=tt[i][:], scalar=sm[:, 1:2], in1=lt[i // 4][:, i % 4, :], op0=ALU.add, op1=ALU.add
                 )
             nc.sync.dma_start(out=o4[i // 4, i % 4], in_=o32[i][:])
+
+        def O16(i, eng=None):
+            if i in PRE:
+                nc.vector.tensor_scalar(out=o16[i][:], in0=perm(tt[i]), scalar1=sh[:], scalar2=None, op0=ALU.add)
+            else:
+                eng(out=o16[i][:], in_=perm(o32[i]))
 
         pt = {}
 
@@ -389,25 +409,30 @@ def tile_regularizationlearningnetworkcoefficient_x1_kernel(
                     out=o2[4 * q : 4 * q + 4, 128 * gd : 128 * gd + 128], in_=psc[gd][32 * q : 32 * q + 4, :].bitcast(I32)
                 )
 
+        vc, sc = nc.vector.tensor_copy, nc.scalar.copy
         O(0)
-        O(1)
-        PT(0, 0)
         O(2)
+        O16(2)
+        O16(0, sc)
+        O(1)
         O(3)
-        PT(0, 1)
-        O(4)
-        PC(0, 0, nc.scalar.copy)
-        O(5)
-        for i in (4, 5):
-            nc.vector.tensor_copy(out=o16[i][:], in_=perm(o32[i]))
-        PT(1, 0)
-        PC(0, 1, nc.scalar.copy)
-        O(6)
+        O16(1, sc)
         O(7)
+        O16(7)
+        O(4)
+        PT(0, 0)
+        O16(3, vc)
+        PC(0, 0, sc)
+        O(5)
+        O16(4, sc)
+        PT(0, 1)
+        O16(5, vc)
+        PC(0, 1, sc)
+        O(6)
+        PT(1, 0)
+        O16(6, vc)
+        PC(1, 0, sc)
         PQ(0)
-        nc.vector.tensor_copy(out=o16[6][:], in_=perm(o32[6]))
-        nc.vector.tensor_copy(out=o16[7][:], in_=perm(o32[7]))
         PT(1, 1)
-        PC(1, 0, nc.scalar.copy)
-        PC(1, 1, nc.vector.tensor_copy)
+        PC(1, 1, vc)
         PQ(1)

@@ -16,6 +16,8 @@ N, D, M = 1024, 1024, 512
 P = 128
 BIG = 2.0**100
 OFF = 2
+VCOL = 320
+V0 = 256
 PRE = (2, 7)
 FLOPS = 2 * 2 * N * D * M
 
@@ -102,10 +104,10 @@ def tile_regularizationlearningnetworkcoefficient_x1_kernel(
         nc.sync.dma_start(out=wt[0][:], in_=w4[0])
         ldx(0)
         nc.sync.dma_start(out=wt[1][:], in_=w4[1])
-        ldx(1)
-        nc.sync.dma_start(out=yt[0][:], in_=y4[0])
-        for i in range(2, 8):
+        for i in range(1, 8):
             ldx(i)
+            if i == 3:
+                nc.sync.dma_start(out=yt[0][:], in_=y4[0])
         nc.sync.dma_start(out=yt[1][:], in_=y4[1])
         nc.sync.dma_start(out=lt[0][:], in_=l4[0])
         nc.sync.dma_start(out=lt[1][:], in_=l4[1])
@@ -147,9 +149,15 @@ def tile_regularizationlearningnetworkcoefficient_x1_kernel(
                 out=xsc[i][:].bitcast(FP8X4), scales=xss[i][:], in_=xsg[i][:].rearrange("p g n t -> p (g n t)")
             )
 
+        def weave(dst, src, vcol=VCOL):
+            for eng, c in ((nc.vector.tensor_copy, slice(0, vcol)), (nc.scalar.copy, slice(vcol, M))):
+                eng(
+                    out=dst[:, c, :].rearrange("p (c i) t -> p c t i", i=4),
+                    in_=src[:, :, c].rearrange("p t (c i) -> p c t i", i=4),
+                )
+
         def WI(g):
-            nc.vector.tensor_copy(out=wg[g][:, 0:256, :], in_=wt[g][:, :, 0:256].rearrange("p t m -> p m t"))
-            nc.scalar.copy(out=wg[g][:, 256:512, :], in_=wt[g][:, :, 256:512].rearrange("p t m -> p m t"))
+            weave(wg[g], wt[g], 320 if g == 0 else 192)
 
         def WQ(g):
             nc.vector.quantize_mx(
@@ -187,8 +195,7 @@ def tile_regularizationlearningnetworkcoefficient_x1_kernel(
             )
 
         def DG(g):
-            nc.vector.tensor_copy(out=dbg[g][:, 0:256, :], in_=dbr[g][:, :, 0:256].rearrange("p t m -> p m t"))
-            nc.scalar.copy(out=dbg[g][:, 256:512, :], in_=dbr[g][:, :, 256:512].rearrange("p t m -> p m t"))
+            weave(dbg[g], dbr[g], (V0, VCOL)[g])
 
         def DQ(g):
             nc.vector.quantize_mx(
@@ -275,8 +282,8 @@ def tile_regularizationlearningnetworkcoefficient_x1_kernel(
         X(0)
         X(1)
         WI(0)
-        XS(0)
         WQ(0)
+        XS(0)
         WI(1)
         XQ(0)
         XS(1)
@@ -307,17 +314,16 @@ def tile_regularizationlearningnetworkcoefficient_x1_kernel(
                 XR()
             if i == 4:
                 XAV()
-            if i == 5:
-                XAQ(0, 0)
             if i == 6:
                 DG(0)
             if i == 7:
                 for k in range(4, 8):
                     SG(k)
             if i == 8:
-                DQ(0)
+                XAQ(0, 0)
             if i == 9:
-                XAQ(0, 1)
+                DQ(0)
+        XAQ(0, 1)
         C(0)
         DG(1)
         S(2)
@@ -404,8 +410,10 @@ def tile_regularizationlearningnetworkcoefficient_x1_kernel(
                 out=pc[gd][:].bitcast(FP8X4), scales=psc[gd][:], in_=pg[gd][:].rearrange("p m t -> p (m t)")
             )
             nc.sync.dma_start(out=o1[:, 512 * gd : 512 * gd + 512], in_=pc[gd][:].bitcast(I32))
+
+        def PS(gd):
             for q in range(4):
-                nc.sync.dma_start(
+                nc.scalar.dma_start(
                     out=o2[4 * q : 4 * q + 4, 128 * gd : 128 * gd + 128], in_=psc[gd][32 * q : 32 * q + 4, :].bitcast(I32)
                 )
 
@@ -434,5 +442,7 @@ def tile_regularizationlearningnetworkcoefficient_x1_kernel(
         PC(1, 0, sc)
         PQ(0)
         PT(1, 1)
+        PS(0)
         PC(1, 1, vc)
         PQ(1)
+        PS(1)

@@ -1,3 +1,4 @@
+import math
 from contextlib import ExitStack
 
 import concourse.mybir as mybir
@@ -14,12 +15,13 @@ ACT = mybir.ActivationFunctionType
 
 N, D, M = 1024, 1024, 512
 P = 128
-BIG = 2.0**100
-OFF = 2
-VCOL = 320
-V0 = 256
-PRE = (2, 7)
 FLOPS = 2 * 2 * N * D * M
+
+STEP = 2.0 / math.sqrt(N)
+TO_SIGN = 2.0**100
+VECTOR_COLUMNS = 320
+SIDE_TILES = (0, 1)
+EARLY_GPSIMD, EARLY_VECTOR = 2, 7
 
 
 def tile_regularizationlearningnetworkcoefficient_x1_kernel(
@@ -28,421 +30,468 @@ def tile_regularizationlearningnetworkcoefficient_x1_kernel(
     nc = tc.nc
     with ExitStack() as ctx:
         keep = ctx.enter_context(tc.tile_pool(name="keep", bufs=1))
-        ps_tp = ctx.enter_context(tc.psum_pool(name="ps_tp", bufs=2))
-        ps_bk = ctx.enter_context(tc.psum_pool(name="ps_bk", bufs=5))
-        ps_sm = ctx.enter_context(tc.psum_pool(name="ps_sm", bufs=1))
-
         roll = ctx.enter_context(tc.tile_pool(name="roll", bufs=4))
+        ps_x = ctx.enter_context(tc.psum_pool(name="ps_x", bufs=2))
+        ps_bank = ctx.enter_context(tc.psum_pool(name="ps_bank", bufs=5))
+        ps_sum = ctx.enter_context(tc.psum_pool(name="ps_sum", bufs=1))
+        ctx.enter_context(tc.manual_schedule())
 
-        def T(name, shape, dt):
+        def tile(name, shape, dt):
             return keep.tile(shape, dt, name=name, align_bytes=64)
 
-        s8 = T("s8", [P, 2, 4], BF16)
-        a8 = T("a8", [P, 2, 4], BF16)
-        b8 = T("b8", [P, 2, 4], BF16)
-        sf = T("sf", [P, 8], F32)
-        af = T("af", [P, 8], F32)
-        bfl = T("bfl", [P, 8], F32)
-        bh = T("bh", [P, 8], F32)
-        nbh = T("nbh", [P, 8], F32)
-        idf = T("idf", [P, P], F32)
-        idb = T("idb", [P, P], BF16)
-        negs = T("negs", [P, P], F32)
-        one = T("one", [P, 1], BF16)
-        diag = T("diag", [P, 8, P], BF16)
-        xt = [T("xt%d" % i, [P, D], BF16) for i in range(8)]
-        wt = [T("wt%d" % g, [P, 4, M], BF16) for g in range(2)]
-        yt = [T("yt%d" % g, [P, 4, M], BF16) for g in range(2)]
-        lt = [T("lt%d" % g, [P, 4, M], BF16) for g in range(2)]
-        wg = [T("wg%d" % g, [P, M, 4], BF16) for g in range(2)]
-        wc = [T("wc%d" % g, [P, M], U32) for g in range(2)]
-        ws = [T("ws%d" % g, [P, M], U8) for g in range(2)]
-        xsc = [T("xsc%d" % i, [P, 2 * P], U32) for i in range(8)]
-        xss = [T("xss%d" % i, [P, 2 * P], U8) for i in range(8)]
-        yb = [T("yb%d" % i, [P, M], F32) for i in range(8)]
-        dbr = [T("dbr%d" % g, [P, 4, M], BF16) for g in range(2)]
-        dbg = [T("dbg%d" % g, [P, M, 4], BF16) for g in range(2)]
-        dbc = [T("dbc%d" % g, [P, M], U32) for g in range(2)]
-        dbs = [T("dbs%d" % g, [P, M], U8) for g in range(2)]
-        xr = T("xr", [P, 4, 512], BF16)
-        xag = [T("xag%d" % g, [P, 2, 4, P, 4], BF16) for g in range(2)]
-        xac = [T("xac%d" % g, [P, D], U32) for g in range(2)]
-        xas = [T("xas%d" % g, [P, D], U8) for g in range(2)]
-        sg = [T("sg%d" % i, [P, M], BF16) for i in range(8)]
-        cc = [T("cc%d" % i, [P, M], F32) for i in range(8)]
-        tt = [T("tt%d" % i, [P, M], F32) for i in range(8)]
-        stats = T("stats", [P, 8], F32)
-        st2 = T("st2", [P, OFF], F32)
-        gs = [T("gs%d" % i, [P, M], F32) for i in range(OFF)]
-        lamst = T("lamst", [P, 2], F32)
-        sh = T("sh", [P, 1], F32)
-        o32 = cc
-        o16 = [T("o16_%d" % i, [P, 2, P, 2], BF16) for i in range(8)]
-        pg = [T("pg%d" % g, [P, 512, 4], BF16) for g in range(2)]
-        pc = [T("pc%d" % g, [P, 512], U32) for g in range(2)]
-        psc = [T("psc%d" % g, [P, 512], U8) for g in range(2)]
+        def tiles(name, count, shape, dt):
+            return [tile(name + str(i), shape, dt) for i in range(count)]
 
-        ctx.enter_context(tc.manual_schedule())
-        xsg, th, ex = {}, {}, {}
+        s_bf = tile("s_bf", [P, 2, 4], BF16)
+        a_bf = tile("a_bf", [P, 2, 4], BF16)
+        b_bf = tile("b_bf", [P, 2, 4], BF16)
+        s_sign = tile("s_sign", [P, 8], F32)
+        a_col = tile("a_col", [P, 8], F32)
+        b_col = tile("b_col", [P, 8], F32)
+        b_half = tile("b_half", [P, 8], F32)
+        b_neg_half = tile("b_neg_half", [P, 1], F32)
+        zero = tile("zero", [P, 1], F32)
+        ident = tile("ident", [P, P], F32)
+        ident_bf = tile("ident_bf", [P, P], BF16)
+        ones_bf = tile("ones_bf", [P, 1], BF16)
+        mean_weights = tile("mean_weights", [P, P], F32)
+        diag_a = tile("diag_a", [P, 8, P], BF16)
+        x_in = tiles("x_in", 8, [P, D], BF16)
+        w_in = tiles("w_in", 2, [P, 4, M], BF16)
+        y_in = tiles("y_in", 2, [P, 4, M], BF16)
+        lam_in = tiles("lam_in", 2, [P, 4, M], BF16)
+        w_mix = tiles("w_mix", 2, [P, M, 4], BF16)
+        w_code = tiles("w_code", 2, [P, M], U32)
+        w_scale = tiles("w_scale", 2, [P, M], U8)
+        xs_code = tiles("xs_code", 8, [P, 2 * P], U32)
+        xs_scale = tiles("xs_scale", 8, [P, 2 * P], U8)
+        yb = tiles("yb", 8, [P, M], F32)
+        db_rows = tiles("db_rows", 2, [P, 4, M], BF16)
+        db_mix = tiles("db_mix", 2, [P, M, 4], BF16)
+        db_code = tiles("db_code", 2, [P, M], U32)
+        db_scale = tiles("db_scale", 2, [P, M], U8)
+        xa_rows = tile("xa_rows", [P, 4, 512], BF16)
+        xa_mix = tiles("xa_mix", 2, [P, 2, 4, P, 4], BF16)
+        xa_code = tiles("xa_code", 2, [P, D], U32)
+        xa_scale = tiles("xa_scale", 2, [P, D], U8)
+        u_big = tiles("u_big", 8, [P, M], BF16)
+        coef = tiles("coef", 8, [P, M], F32)
+        out_rows = coef
+        step = tiles("step", 8, [P, M], F32)
+        side = tiles("side", len(SIDE_TILES), [P, M], F32)
+        row_sum = tile("row_sum", [P, 8], F32)
+        side_sum = tile("side_sum", [P, len(SIDE_TILES)], F32)
+        lam_sum = tile("lam_sum", [P, 2], F32)
+        shift = tile("shift", [P, 1], F32)
+        out_bf = tiles("out_bf", 8, [P, 2, P, 2], BF16)
+        out_mix = tiles("out_mix", 2, [P, 512, 4], BF16)
+        out_code = tiles("out_code", 2, [P, 512], U32)
+        out_scale = tiles("out_scale", 2, [P, 512], U8)
+        xs_mix, tanh_z, exp_lam, x_turned, bank = {}, {}, {}, {}, {}
 
-        def vec(v):
-            return v.rearrange("(g p t) -> p g t", g=2, t=4)
+        def columns(vec):
+            return vec.rearrange("(g p t) -> p g t", g=2, t=4)
 
-        nc.scalar.dma_start(out=s8[:], in_=vec(s))
-        nc.gpsimd.dma_start(out=a8[:], in_=vec(a))
-        nc.scalar.dma_start(out=b8[:], in_=vec(b))
-        nc.vector.memset(sh[:], 0.0)
-        nc.scalar.activation(out=sh[:], in_=sh[:], func=ACT.Tanh)
-        x4 = x.rearrange("(g p t) d -> g t p d", g=2, t=4)
-        w4 = w.rearrange("(g p t) m -> g p t m", g=2, t=4)
-        y4 = y.rearrange("(g p t) m -> g p t m", g=2, t=4)
-        l4 = lam.rearrange("(g p t) m -> g p t m", g=2, t=4)
+        nc.scalar.dma_start(out=s_bf[:], in_=columns(s))
+        nc.gpsimd.dma_start(out=a_bf[:], in_=columns(a))
+        nc.scalar.dma_start(out=b_bf[:], in_=columns(b))
+        nc.vector.memset(zero[:], 0.0)
+        nc.scalar.activation(out=zero[:], in_=zero[:], func=ACT.Tanh)
 
-        def ldx(i):
-            nc.sync.dma_start(out=xt[i][:], in_=x4[i // 4, i % 4])
+        x_hbm = x.rearrange("(g p t) d -> g t p d", g=2, t=4)
+        w_hbm = w.rearrange("(g p t) m -> g p t m", g=2, t=4)
+        y_hbm = y.rearrange("(g p t) m -> g p t m", g=2, t=4)
+        lam_hbm = lam.rearrange("(g p t) m -> g p t m", g=2, t=4)
 
-        nc.sync.dma_start(out=wt[0][:], in_=w4[0])
-        ldx(0)
-        nc.sync.dma_start(out=wt[1][:], in_=w4[1])
-        for i in range(1, 8):
-            ldx(i)
-            if i == 3:
-                nc.sync.dma_start(out=yt[0][:], in_=y4[0])
-        nc.sync.dma_start(out=yt[1][:], in_=y4[1])
-        nc.sync.dma_start(out=lt[0][:], in_=l4[0])
-        nc.sync.dma_start(out=lt[1][:], in_=l4[1])
+        def load_x(i):
+            nc.sync.dma_start(out=x_in[i][:], in_=x_hbm[i // 4, i % 4])
 
-        make_identity(nc, idf[:])
-        nc.gpsimd.tensor_copy(out=idb[:], in_=idf[:])
-        nc.gpsimd.memset(negs[:], -1.0 / (D * M))
-        nc.gpsimd.memset(one[:], 1.0)
-        nc.gpsimd.memset(lamst[:, 1:2], float(D * M // P))
-        fl = lambda t: t[:].rearrange("p g t -> p (g t)")
-        nc.gpsimd.tensor_scalar(out=sf[:], in0=fl(s8), scalar1=BIG, scalar2=0.0, op0=ALU.mult, op1=ALU.add)
-        nc.gpsimd.tensor_copy(out=af[:], in_=fl(a8))
-        nc.gpsimd.tensor_copy(out=bfl[:], in_=fl(b8))
-        nc.gpsimd.tensor_scalar(out=bh[:], in0=fl(b8), scalar1=0.5, scalar2=0.0, op0=ALU.mult, op1=ALU.add)
-        nc.gpsimd.tensor_scalar(out=nbh[:], in0=fl(b8), scalar1=-0.5, scalar2=0.0, op0=ALU.mult, op1=ALU.add)
+        nc.sync.dma_start(out=w_in[0][:], in_=w_hbm[0])
+        load_x(0)
+        nc.sync.dma_start(out=w_in[1][:], in_=w_hbm[1])
+        load_x(1)
+        load_x(2)
+        nc.sync.dma_start(out=y_in[0][:], in_=y_hbm[0])
+        for i in range(3, 8):
+            load_x(i)
+        nc.sync.dma_start(out=y_in[1][:], in_=y_hbm[1])
+        nc.sync.dma_start(out=lam_in[0][:], in_=lam_hbm[0])
+        nc.sync.dma_start(out=lam_in[1][:], in_=lam_hbm[1])
 
-        tp = {}
-        bank = {}
+        def flat(cols):
+            return cols[:].rearrange("p g t -> p (g t)")
 
-        def X(i):
-            t_ = ps_tp.tile([P, 2, 2, P], F32, name="tp")
-            tp[i] = t_
-            words = xt[i][:].bitcast(F32)
-            for gd in range(2):
-                for u in range(2):
-                    nc.tensor.transpose(t_[:, gd, u, :], words[:, 256 * gd + u : 256 * (gd + 1) : 2], idf[:])
+        make_identity(nc, ident[:])
+        nc.gpsimd.tensor_copy(out=ident_bf[:], in_=ident[:])
+        nc.gpsimd.memset(mean_weights[:], -1.0 / (D * M))
+        nc.gpsimd.memset(ones_bf[:], 1.0)
+        nc.gpsimd.memset(lam_sum[:, 1:2], float(D * M // P))
+        nc.gpsimd.tensor_scalar(
+            out=s_sign[:], in0=flat(s_bf), scalar1=TO_SIGN, scalar2=0.0, op0=ALU.mult, op1=ALU.add
+        )
+        nc.gpsimd.tensor_copy(out=a_col[:], in_=flat(a_bf))
+        nc.gpsimd.tensor_copy(out=b_col[:], in_=flat(b_bf))
+        nc.gpsimd.tensor_scalar(out=b_half[:], in0=flat(b_bf), scalar1=0.5, scalar2=0.0, op0=ALU.mult, op1=ALU.add)
+        nc.gpsimd.tensor_scalar(
+            out=b_neg_half[:], in0=flat(b_bf)[:, 0:1], scalar1=-0.5, scalar2=0.0, op0=ALU.mult, op1=ALU.add
+        )
 
-        def XS(i):
-            xsg[i] = roll.tile([P, 2, P, 4], BF16, name="xsg", align_bytes=64)
-            for gd in range(2):
-                src = tp[i][:, gd].bitcast(BF16).rearrange("p u (n e) -> p n u e", e=2)
-                fac = s8[:, gd, :].unsqueeze(1).to_broadcast([P, P, 4]).rearrange("p n (u e) -> p n u e", e=2)
-                nc.vector.tensor_tensor(
-                    out=xsg[i][:, gd].rearrange("p n (u e) -> p n u e", e=2), in0=src, in1=fac, op=ALU.mult
-                )
+        def quantise(code, scale, mixed):
+            nc.vector.quantize_mx(out=code.bitcast(FP8X4), scales=scale, in_=mixed)
 
-        def XQ(i):
-            nc.vector.quantize_mx(
-                out=xsc[i][:].bitcast(FP8X4), scales=xss[i][:], in_=xsg[i][:].rearrange("p g n t -> p (g n t)")
-            )
-
-        def weave(dst, src, vcol=VCOL):
-            for eng, c in ((nc.vector.tensor_copy, slice(0, vcol)), (nc.scalar.copy, slice(vcol, M))):
-                eng(
+        def interleave(dst, src):
+            for copy, c in (
+                (nc.vector.tensor_copy, slice(0, VECTOR_COLUMNS)),
+                (nc.scalar.copy, slice(VECTOR_COLUMNS, M)),
+            ):
+                copy(
                     out=dst[:, c, :].rearrange("p (c i) t -> p c t i", i=4),
                     in_=src[:, :, c].rearrange("p t (c i) -> p c t i", i=4),
                 )
 
-        def WI(g):
-            weave(wg[g], wt[g], 320 if g == 0 else 192)
+        def quantise_w(g):
+            quantise(w_code[g][:], w_scale[g][:], w_mix[g][:].rearrange("p m t -> p (m t)"))
 
-        def WQ(g):
-            nc.vector.quantize_mx(
-                out=wc[g][:].bitcast(FP8X4), scales=ws[g][:], in_=wg[g][:].rearrange("p m t -> p (m t)")
-            )
+        def turn_x(i):
+            x_turned[i] = ps_x.tile([P, 2, 2, P], F32, name="x_turned")
+            words = x_in[i][:].bitcast(F32)
+            for g in range(2):
+                for u in range(2):
+                    nc.tensor.transpose(
+                        x_turned[i][:, g, u, :], words[:, 256 * g + u : 256 * (g + 1) : 2], ident[:]
+                    )
 
-        def Z(i):
-            z_ = ps_bk.tile([P, M], F32, name="bk")
-            bank["z", i] = z_
-            for gd in range(2):
-                c = slice(gd * P, gd * P + P)
-                nc.tensor.matmul_mx(
-                    out=z_[:], lhsT=xsc[i][:, c].bitcast(FP8X4), lhsT_scale=xss[i][:, c],
-                    rhs=wc[gd][:].bitcast(FP8X4), rhs_scale=ws[gd][:], start=(gd == 0), stop=(gd == 1),
+        def scale_x(i):
+            xs_mix[i] = roll.tile([P, 2, P, 4], BF16, name="xs_mix", align_bytes=64)
+            for g in range(2):
+                factor = s_bf[:, g, :].unsqueeze(1).to_broadcast([P, P, 4])
+                nc.vector.tensor_tensor(
+                    out=xs_mix[i][:, g].rearrange("p n (u e) -> p n u e", e=2),
+                    in0=x_turned[i][:, g].bitcast(BF16).rearrange("p u (n e) -> p n u e", e=2),
+                    in1=factor.rearrange("p n (u e) -> p n u e", e=2),
+                    op=ALU.mult,
                 )
 
-        def TH(i):
-            th[i] = roll.tile([P, M], F32, name="th", align_bytes=64)
-            nc.scalar.activation(out=th[i][:], in_=bank["z", i][:], func=ACT.Tanh, scale=0.5)
+        def quantise_xs(i):
+            quantise(xs_code[i][:], xs_scale[i][:], xs_mix[i][:].rearrange("p g n t -> p (g n t)"))
 
-        def YB(i):
-            nc.gpsimd.tensor_scalar(
-                out=yb[i][:], in0=yt[i // 4][:, i % 4, :], scalar1=-0.5, scalar2=bfl[:, i : i + 1],
-                op0=ALU.add, op1=ALU.mult,
-            )
+        def logits(i):
+            z = ps_bank.tile([P, M], F32, name="bank")
+            bank["z", i] = z
+            for g in range(2):
+                c = slice(P * g, P * g + P)
+                nc.tensor.matmul_mx(
+                    out=z[:],
+                    lhsT=xs_code[i][:, c].bitcast(FP8X4),
+                    lhsT_scale=xs_scale[i][:, c],
+                    rhs=w_code[g][:].bitcast(FP8X4),
+                    rhs_scale=w_scale[g][:],
+                    start=(g == 0),
+                    stop=(g == 1),
+                )
 
-        def DI(g):
-            for k in range(4 * g, 4 * g + 4):
-                nc.scalar.activation(out=diag[:, k, :], in_=idb[:], func=ACT.Copy, scale=af[:, k : k + 1])
+        def tanh_half(i):
+            tanh_z[i] = roll.tile([P, M], F32, name="tanh_z", align_bytes=64)
+            nc.scalar.activation(out=tanh_z[i][:], in_=bank["z", i][:], func=ACT.Tanh, scale=0.5)
 
-        def DB(i):
+        def scale_y(i):
+            source = y_in[i // 4][:, i % 4, :]
+            if i == 0:
+                nc.scalar.activation(
+                    out=yb[i][:], in_=source, func=ACT.Identity, scale=b_col[:, 0:1], bias=b_neg_half[:]
+                )
+            else:
+                nc.gpsimd.tensor_scalar(
+                    out=yb[i][:], in0=source, scalar1=-0.5, scalar2=b_col[:, i : i + 1], op0=ALU.add, op1=ALU.mult
+                )
+
+        def residual(i):
             nc.vector.scalar_tensor_tensor(
-                out=dbr[i // 4][:, i % 4, :], in0=th[i][:], scalar=bh[:, i : i + 1], in1=yb[i][:],
-                op0=ALU.mult, op1=ALU.subtract,
+                out=db_rows[i // 4][:, i % 4, :],
+                in0=tanh_z[i][:],
+                scalar=b_half[:, i : i + 1],
+                in1=yb[i][:],
+                op0=ALU.mult,
+                op1=ALU.subtract,
             )
 
-        def DG(g):
-            weave(dbg[g], dbr[g], (V0, VCOL)[g])
+        def quantise_db(g):
+            quantise(db_code[g][:], db_scale[g][:], db_mix[g][:].rearrange("p m t -> p (m t)"))
 
-        def DQ(g):
-            nc.vector.quantize_mx(
-                out=dbc[g][:].bitcast(FP8X4), scales=dbs[g][:], in_=dbg[g][:].rearrange("p m t -> p (m t)")
-            )
-
-        def XR():
+        def scale_xa_rows():
             for t in range(4):
                 nc.vector.tensor_scalar(
-                    out=xr[:, t, :], in0=xt[t][:, 0:512], scalar1=af[:, t : t + 1], scalar2=None, op0=ALU.mult
+                    out=xa_rows[:, t, :], in0=x_in[t][:, 0:512], scalar1=a_col[:, t : t + 1], scalar2=None, op0=ALU.mult
                 )
 
-        def XAV():
-            for eng, j0 in ((nc.vector.tensor_copy, 0), (nc.scalar.copy, 2)):
-                eng(
-                    out=xag[0][:, 0, j0 : j0 + 2],
-                    in_=xr[:].rearrange("p t (q j) -> p j q t", j=4)[:, j0 : j0 + 2],
-                )
+        def interleave_xa_rows():
+            source = xa_rows[:].rearrange("p t (q j) -> p j q t", j=4)
+            nc.vector.tensor_copy(out=xa_mix[0][:, 0, 0:2], in_=source[:, 0:2])
+            nc.scalar.copy(out=xa_mix[0][:, 0, 2:4], in_=source[:, 2:4])
 
-        def XA(g, dc):
-            k_ = ps_bk.tile([P, 4, P], F32, name="bk")
+        def diagonals(g):
+            for i in range(4 * g, 4 * g + 4):
+                nc.scalar.activation(out=diag_a[:, i, :], in_=ident_bf[:], func=ACT.Copy, scale=a_col[:, i : i + 1])
+
+        def make_xa(g, chunk):
+            product = ps_bank.tile([P, 4, P], F32, name="bank")
             for t in range(4):
                 nc.tensor.matmul(
-                    out=k_[:, t, :], lhsT=diag[:, 4 * g + t, :], rhs=xt[4 * g + t][:, P * dc : P * dc + P],
-                    start=True, stop=True,
+                    out=product[:, t, :],
+                    lhsT=diag_a[:, 4 * g + t, :],
+                    rhs=x_in[4 * g + t][:, P * chunk : P * chunk + P],
+                    start=True,
+                    stop=True,
                 )
-            r = 32 * (dc % 4)
+            q0 = 32 * (chunk % 4)
             nc.scalar.copy(
-                out=xag[g][:, dc // 4, :, r : r + 32, :], in_=k_[:].rearrange("p t (q j) -> p j q t", j=4)
+                out=xa_mix[g][:, chunk // 4, :, q0 : q0 + 32, :],
+                in_=product[:].rearrange("p t (q j) -> p j q t", j=4),
             )
 
-        def XAQ(g, gd):
-            c = slice(512 * gd, 512 * gd + 512)
-            nc.vector.quantize_mx(
-                out=xac[g][:, c].bitcast(FP8X4), scales=xas[g][:, c],
-                in_=xag[g][:, gd].rearrange("p j q t -> p (j q t)"),
-            )
+        def quantise_xa(g, half):
+            c = slice(512 * half, 512 * half + 512)
+            quantise(xa_code[g][:, c], xa_scale[g][:, c], xa_mix[g][:, half].rearrange("p j q t -> p (j q t)"))
 
-        def SG(i):
+        def enlarge_u(i):
             nc.vector.tensor_scalar(
-                out=sg[i][:], in0=wt[i // 4][:, i % 4, :], scalar1=sf[:, i : i + 1], scalar2=1.0,
-                op0=ALU.mult, op1=ALU.min,
+                out=u_big[i][:],
+                in0=w_in[i // 4][:, i % 4, :],
+                scalar1=s_sign[:, i : i + 1],
+                scalar2=1.0,
+                op0=ALU.mult,
+                op1=ALU.min,
             )
 
-        def EX(i):
-            ex[i] = roll.tile([P, M], F32, name="ex", align_bytes=64)
-            nc.scalar.activation(out=ex[i][:], in_=lt[i // 4][:, i % 4, :], func=ACT.Exp)
+        def exponential(i):
+            exp_lam[i] = roll.tile([P, M], F32, name="exp_lam", align_bytes=64)
+            nc.scalar.activation(out=exp_lam[i][:], in_=lam_in[i // 4][:, i % 4, :], func=ACT.Exp, bias=zero[:])
 
-        def C(i):
+        def coefficient(i):
             nc.vector.scalar_tensor_tensor(
-                out=cc[i][:], in0=sg[i][:], scalar=-1.0, in1=ex[i][:], op0=ALU.max, op1=ALU.mult
+                out=coef[i][:], in0=u_big[i][:], scalar=-1.0, in1=exp_lam[i][:], op0=ALU.max, op1=ALU.mult
             )
 
-        def GR(i):
-            g_ = ps_bk.tile([P, M], F32, name="bk")
-            bank["g", i] = g_
+        def gradient(i):
+            grad = ps_bank.tile([P, M], F32, name="bank")
+            bank["grad", i] = grad
             c = slice(P * i, P * i + P)
             for g in range(2):
                 nc.tensor.matmul_mx(
-                    out=g_[:], lhsT=xac[g][:, c].bitcast(FP8X4), lhsT_scale=xas[g][:, c],
-                    rhs=dbc[g][:].bitcast(FP8X4), rhs_scale=dbs[g][:], start=(g == 0), stop=(g == 1),
+                    out=grad[:],
+                    lhsT=xa_code[g][:, c].bitcast(FP8X4),
+                    lhsT_scale=xa_scale[g][:, c],
+                    rhs=db_code[g][:].bitcast(FP8X4),
+                    rhs_scale=db_scale[g][:],
+                    start=(g == 0),
+                    stop=(g == 1),
                 )
 
-        def NN(i):
+        def make_step(i):
             nc.vector.scalar_tensor_tensor(
-                out=tt[i][:], in0=bank["g", i][:], scalar=1.0 / 16.0, in1=cc[i][:], op0=ALU.mult, op1=ALU.mult,
-                accum_out=stats[:, i : i + 1],
+                out=step[i][:],
+                in0=bank["grad", i][:],
+                scalar=STEP,
+                in1=coef[i][:],
+                op0=ALU.mult,
+                op1=ALU.mult,
+                accum_out=row_sum[:, i : i + 1],
             )
 
-        others = [lambda i=i: YB(i) for i in range(2)]
-        others += [lambda: XA(0, 4), lambda: YB(2), lambda: XA(0, 5), lambda: YB(3)]
-        others += [lambda: XA(0, 6), lambda: YB(4), lambda: XA(0, 7), lambda: YB(5)]
-        others += [lambda: XA(1, 0), lambda: YB(6), lambda: XA(1, 1), lambda: YB(7)]
-        others += [lambda: XA(1, 2), lambda: EX(0), lambda: XA(1, 3)]
-        others += [lambda: EX(1), lambda: XA(1, 4), lambda: EX(2), lambda: XA(1, 5)]
-        others += [lambda: EX(3), lambda: XA(1, 6), lambda: EX(4), lambda: XA(1, 7)]
-        others += [lambda i=i: EX(i) for i in range(5, 8)]
+        chunks = [(0, k) for k in range(4, 8)] + [(1, k) for k in range(8)]
+        todo = [lambda: scale_y(0)]
+        for k in range(7):
+            todo += [lambda k=k: scale_y(k + 1), lambda k=k: make_xa(*chunks[k])]
+        for k in range(5):
+            todo += [lambda k=k: exponential(k), lambda k=k: make_xa(*chunks[7 + k])]
+        todo += [lambda k=k: exponential(k) for k in range(5, 8)]
 
-        def S(n):
-            for k in range(n):
-                if others:
-                    others.pop(0)()
+        def take(count):
+            for item in todo[:count]:
+                item()
+            for item in todo[:count]:
+                todo.remove(item)
 
-        X(0)
-        X(1)
-        WI(0)
-        WQ(0)
-        XS(0)
-        WI(1)
-        XQ(0)
-        XS(1)
-        WQ(1)
-        DI(0)
-        S(1)
-        DI(1)
-        XQ(1)
-        X(2)
-        for k in range(4):
-            SG(k)
+        turn_x(0)
+        turn_x(1)
+        interleave(w_mix[0], w_in[0])
+        quantise_w(0)
+        scale_x(0)
+        interleave(w_mix[1], w_in[1])
+        quantise_xs(0)
+        scale_x(1)
+        quantise_w(1)
+        diagonals(0)
+        take(1)
+        diagonals(1)
+        quantise_xs(1)
+        turn_x(2)
         for i in range(1, 11):
             if i <= 8:
-                Z(i - 1)
+                logits(i - 1)
             if 2 <= i < 8:
-                XS(i)
+                scale_x(i)
                 if i < 7:
-                    X(i + 1)
+                    turn_x(i + 1)
             if i <= 8:
-                TH(i - 1)
+                tanh_half(i - 1)
             if i >= 3:
-                DB(i - 3)
+                residual(i - 3)
             if 2 <= i < 8:
-                XQ(i)
+                quantise_xs(i)
             if i <= 9:
-                S(2)
+                take(2)
+            if i == 1:
+                for k in range(4):
+                    enlarge_u(k)
             if i == 3:
-                XR()
+                scale_xa_rows()
             if i == 4:
-                XAV()
+                interleave_xa_rows()
             if i == 6:
-                DG(0)
+                interleave(db_mix[0], db_rows[0])
             if i == 7:
                 for k in range(4, 8):
-                    SG(k)
+                    enlarge_u(k)
             if i == 8:
-                XAQ(0, 0)
+                quantise_xa(0, 0)
             if i == 9:
-                DQ(0)
-        XAQ(0, 1)
-        C(0)
-        DG(1)
-        S(2)
-        S(19)
-        C(1)
-        DQ(1)
-        C(2)
-        XAQ(1, 0)
-        C(3)
-        sm = ps_sm.tile([P, 2], F32, name="sm")
+                quantise_db(0)
+
+        quantise_xa(0, 1)
+        coefficient(0)
+        interleave(db_mix[1], db_rows[1])
+        take(len(todo))
+        coefficient(1)
+        quantise_db(1)
+        coefficient(2)
+        quantise_xa(1, 0)
+        coefficient(3)
+
+        sums = ps_sum.tile([P, 2], F32, name="sums")
         for k in range(32):
             nc.tensor.matmul(
-                out=sm[:, 0:1], lhsT=lt[k // 16][:, (k // 4) % 4, P * (k % 4) : P * (k % 4) + P], rhs=one[:],
-                start=(k == 0), stop=(k == 31),
+                out=sums[:, 0:1],
+                lhsT=lam_in[k // 16][:, (k // 4) % 4, P * (k % 4) : P * (k % 4) + P],
+                rhs=ones_bf[:],
+                start=(k == 0),
+                stop=(k == 31),
             )
-
-        def SUM(i):
-            src = (lamst[:, 0:1] if i == -1 else lamst[:, 1:2]) if i < 0 else (st2 if i < OFF else stats)[:, i : i + 1]
-            nc.tensor.matmul(out=sm[:, 1:2], lhsT=negs[:], rhs=src, start=(i == -2), stop=(i == 7))
-
-        C(4)
-        XAQ(1, 1)
-        nc.vector.tensor_copy(out=lamst[:, 0:1], in_=sm[:, 0:1])
+        coefficient(4)
+        quantise_xa(1, 1)
+        nc.vector.tensor_copy(out=lam_sum[:, 0:1], in_=sums[:, 0:1])
         for i in range(4):
-            GR(i)
+            gradient(i)
         for i in range(5, 8):
-            C(i)
-        for i in range(OFF):
-            nc.scalar.activation(out=gs[i][:], in_=bank["g", i][:], func=ACT.Copy, scale=1.0 / 16.0)
-        for i in range(OFF):
-            nc.gpsimd.tensor_tensor(out=tt[i][:], in0=gs[i][:], in1=cc[i][:], op=ALU.mult)
-            nc.scalar.activation(out=gs[i][:], in_=tt[i][:], func=ACT.Identity, accum_out=st2[:, i : i + 1])
-        for i in range(OFF, 8):
-            NN(i)
-            if 4 <= i + 4 - OFF < 8:
-                GR(i + 4 - OFF)
-            if i in PRE:
-                (nc.vector if i == 7 else nc.gpsimd).tensor_tensor(
-                    out=tt[i][:], in0=tt[i][:], in1=lt[i // 4][:, i % 4, :], op=ALU.add
-                )
-        for i in (-2, -1, 2, 3, 0, 4, 5, 1, 6, 7):
-            SUM(i)
+            coefficient(i)
+        for i in SIDE_TILES:
+            nc.scalar.activation(out=side[i][:], in_=bank["grad", i][:], func=ACT.Copy, scale=STEP)
+        for i in SIDE_TILES:
+            nc.gpsimd.tensor_tensor(out=step[i][:], in0=side[i][:], in1=coef[i][:], op=ALU.mult)
+            nc.scalar.activation(out=side[i][:], in_=step[i][:], func=ACT.Identity, accum_out=side_sum[:, i : i + 1])
+        for i in range(len(SIDE_TILES), 8):
+            make_step(i)
+            if i + 2 < 8:
+                gradient(i + 2)
+            if i in (EARLY_GPSIMD, EARLY_VECTOR):
+                engine = nc.gpsimd if i == EARLY_GPSIMD else nc.vector
+                engine.tensor_tensor(out=step[i][:], in0=step[i][:], in1=lam_in[i // 4][:, i % 4, :], op=ALU.add)
 
-        o4 = out_0.rearrange("(g p t) m -> g t p m", g=2, t=4)
-        o1 = out_1.rearrange("g p m t -> (g p) (m t)").bitcast(I32)
-        o2 = out_2.rearrange("g q m -> (g q) m").bitcast(I32)
+        parts = [lam_sum[:, 1:2], lam_sum[:, 0:1]]
+        for i in (2, 3, 0, 4, 5, 1, 6, 7):
+            parts.append((side_sum if i in SIDE_TILES else row_sum)[:, i : i + 1])
+        for k, part in enumerate(parts):
+            nc.tensor.matmul(
+                out=sums[:, 1:2], lhsT=mean_weights[:], rhs=part, start=(k == 0), stop=(k == len(parts) - 1)
+            )
+        nc.vector.tensor_copy(out=shift[:], in_=sums[:, 1:2])
 
-        def perm(t_):
-            return t_[:].rearrange("p (q u e) -> p u q e", u=2, e=2)
+        out_hbm = out_0.rearrange("(g p t) m -> g t p m", g=2, t=4)
+        code_hbm = out_1.rearrange("g p m t -> (g p) (m t)").bitcast(I32)
+        scale_hbm = out_2.rearrange("g q m -> (g q) m").bitcast(I32)
 
-        nc.vector.tensor_copy(out=sh[:], in_=sm[:, 1:2])
-
-        def O(i):
-            if i in PRE:
-                nc.scalar.activation(out=o32[i][:], in_=tt[i][:], func=ACT.Identity, bias=sh[:])
+        def result(i):
+            if i in (EARLY_GPSIMD, EARLY_VECTOR):
+                nc.scalar.activation(out=out_rows[i][:], in_=step[i][:], func=ACT.Identity, bias=shift[:])
             else:
                 nc.vector.scalar_tensor_tensor(
-                    out=o32[i][:], in0=tt[i][:], scalar=sm[:, 1:2], in1=lt[i // 4][:, i % 4, :], op0=ALU.add, op1=ALU.add
+                    out=out_rows[i][:],
+                    in0=step[i][:],
+                    scalar=sums[:, 1:2],
+                    in1=lam_in[i // 4][:, i % 4, :],
+                    op0=ALU.add,
+                    op1=ALU.add,
                 )
-            nc.sync.dma_start(out=o4[i // 4, i % 4], in_=o32[i][:])
+            nc.sync.dma_start(out=out_hbm[i // 4, i % 4], in_=out_rows[i][:])
 
-        def O16(i, eng=None):
-            if i in PRE:
-                nc.vector.tensor_scalar(out=o16[i][:], in0=perm(tt[i]), scalar1=sh[:], scalar2=None, op0=ALU.add)
-            else:
-                eng(out=o16[i][:], in_=perm(o32[i]))
+        def word_order(rows):
+            return rows[:].rearrange("p (q u e) -> p u q e", u=2, e=2)
 
-        pt = {}
-
-        def PT(gd, jh):
-            p_ = ps_tp.tile([P, 2, 2, P], F32, name="tp")
-            pt[gd, jh] = p_
-            for jj in range(2):
-                words = o16[4 * gd + 2 * jh + jj][:].rearrange("p u q e -> p (u q e)").bitcast(F32)
-                for u in range(2):
-                    nc.tensor.transpose(p_[:, jj, u, :], words[:, P * u : P * u + P], idf[:])
-
-        def PC(gd, jh, eng):
-            dst = pg[gd][:].rearrange("p m t -> p (m t)").bitcast(F32).rearrange("p (q j u) -> p q j u", j=4, u=2)
-            eng(out=dst[:, :, 2 * jh : 2 * jh + 2, :], in_=pt[gd, jh][:].rearrange("p j u q -> p q j u"))
-
-        def PQ(gd):
-            nc.vector.quantize_mx(
-                out=pc[gd][:].bitcast(FP8X4), scales=psc[gd][:], in_=pg[gd][:].rearrange("p m t -> p (m t)")
+        def round_early(i):
+            nc.vector.tensor_scalar(
+                out=out_bf[i][:], in0=word_order(step[i]), scalar1=shift[:], scalar2=None, op0=ALU.add
             )
-            nc.sync.dma_start(out=o1[:, 512 * gd : 512 * gd + 512], in_=pc[gd][:].bitcast(I32))
 
-        def PS(gd):
+        def round_rows(i, copy):
+            copy(out=out_bf[i][:], in_=word_order(out_rows[i]))
+
+        turned = {}
+
+        def turn_result(*which):
+            for i in which:
+                if i // 2 not in turned:
+                    pair = ps_bank.tile([P, 2, 2, P], F32, name="bank")
+                    turned[i // 2] = pair
+                words = out_bf[i][:].rearrange("p u q e -> p (u q e)").bitcast(F32)
+                for u in range(2):
+                    nc.tensor.transpose(turned[i // 2][:, i % 2, u, :], words[:, P * u : P * u + P], ident[:])
+
+        def place_pair(k, copy):
+            words = out_mix[k // 2][:].rearrange("p m t -> p (m t)").bitcast(F32)
+            t0 = 2 * (k % 2)
+            copy(
+                out=words.rearrange("p (q t u) -> p q t u", t=4, u=2)[:, :, t0 : t0 + 2, :],
+                in_=turned[k][:].rearrange("p t u q -> p q t u"),
+            )
+
+        def quantise_result(g):
+            quantise(out_code[g][:], out_scale[g][:], out_mix[g][:].rearrange("p m t -> p (m t)"))
+            nc.sync.dma_start(out=code_hbm[:, 512 * g : 512 * g + 512], in_=out_code[g][:].bitcast(I32))
+
+        def store_scales(g):
             for q in range(4):
                 nc.scalar.dma_start(
-                    out=o2[4 * q : 4 * q + 4, 128 * gd : 128 * gd + 128], in_=psc[gd][32 * q : 32 * q + 4, :].bitcast(I32)
+                    out=scale_hbm[4 * q : 4 * q + 4, P * g : P * g + P],
+                    in_=out_scale[g][32 * q : 32 * q + 4, :].bitcast(I32),
                 )
 
-        vc, sc = nc.vector.tensor_copy, nc.scalar.copy
-        O(0)
-        O(2)
-        O16(2)
-        O16(0, sc)
-        O(1)
-        O(3)
-        O16(1, sc)
-        O(7)
-        O16(7)
-        O(4)
-        PT(0, 0)
-        O16(3, vc)
-        PC(0, 0, sc)
-        O(5)
-        O16(4, sc)
-        PT(0, 1)
-        O16(5, vc)
-        PC(0, 1, sc)
-        O(6)
-        PT(1, 0)
-        O16(6, vc)
-        PC(1, 0, sc)
-        PQ(0)
-        PT(1, 1)
-        PS(0)
-        PC(1, 1, vc)
-        PQ(1)
-        PS(1)
+        by_vector, by_scalar = nc.vector.tensor_copy, nc.scalar.copy
+        result(0)
+        result(2)
+        round_early(2)
+        round_rows(0, by_scalar)
+        result(1)
+        result(3)
+        round_rows(1, by_scalar)
+        result(7)
+        round_early(7)
+        result(4)
+        turn_result(0, 1)
+        round_rows(3, by_vector)
+        place_pair(0, by_scalar)
+        result(5)
+        round_rows(4, by_scalar)
+        turn_result(2, 3)
+        turn_result(7)
+        round_rows(5, by_vector)
+        place_pair(1, by_scalar)
+        result(6)
+        turn_result(4, 5)
+        round_rows(6, by_vector)
+        place_pair(2, by_scalar)
+        quantise_result(0)
+        turn_result(6)
+        store_scales(0)
+        place_pair(3, by_vector)
+        quantise_result(1)
+        store_scales(1)

import math
from contextlib import ExitStack

import concourse.mybir as mybir
from concourse.masks import make_identity

F32 = mybir.dt.float32
BF16 = mybir.dt.bfloat16
U32 = mybir.dt.uint32
I32 = mybir.dt.int32
U8 = mybir.dt.uint8
FP8X4 = mybir.dt.float8_e4m3fn_x4
ALU = mybir.AluOpType
ACT = mybir.ActivationFunctionType

N, D, M = 1024, 1024, 512
P = 128
FLOPS = 2 * 2 * N * D * M

STEP = 2.0 / math.sqrt(N)
TO_SIGN = 2.0**100
VECTOR_COLUMNS = 320
SIDE_TILES = (0, 1)
EARLY_GPSIMD, EARLY_VECTOR = 2, 7


def tile_regularizationlearningnetworkcoefficient_x1_kernel(
    tc, x, s, w, y, a, b, lam, out_0, out_1, out_2
):
    nc = tc.nc
    with ExitStack() as ctx:
        keep = ctx.enter_context(tc.tile_pool(name="keep", bufs=1))
        roll = ctx.enter_context(tc.tile_pool(name="roll", bufs=4))
        ps_x = ctx.enter_context(tc.psum_pool(name="ps_x", bufs=2))
        ps_bank = ctx.enter_context(tc.psum_pool(name="ps_bank", bufs=5))
        ps_sum = ctx.enter_context(tc.psum_pool(name="ps_sum", bufs=1))
        ctx.enter_context(tc.manual_schedule())

        def tile(name, shape, dt):
            return keep.tile(shape, dt, name=name, align_bytes=64)

        def tiles(name, count, shape, dt):
            return [tile(name + str(i), shape, dt) for i in range(count)]

        s_bf = tile("s_bf", [P, 2, 4], BF16)
        a_bf = tile("a_bf", [P, 2, 4], BF16)
        b_bf = tile("b_bf", [P, 2, 4], BF16)
        s_sign = tile("s_sign", [P, 8], F32)
        a_col = tile("a_col", [P, 8], F32)
        b_col = tile("b_col", [P, 8], F32)
        b_half = tile("b_half", [P, 8], F32)
        b_neg_half = tile("b_neg_half", [P, 1], F32)
        zero = tile("zero", [P, 1], F32)
        ident = tile("ident", [P, P], F32)
        ident_bf = tile("ident_bf", [P, P], BF16)
        ones_bf = tile("ones_bf", [P, 1], BF16)
        mean_weights = tile("mean_weights", [P, P], F32)
        diag_a = tile("diag_a", [P, 8, P], BF16)
        x_in = tiles("x_in", 8, [P, D], BF16)
        w_in = tiles("w_in", 2, [P, 4, M], BF16)
        y_in = tiles("y_in", 2, [P, 4, M], BF16)
        lam_in = tiles("lam_in", 2, [P, 4, M], BF16)
        w_mix = tiles("w_mix", 2, [P, M, 4], BF16)
        w_code = tiles("w_code", 2, [P, M], U32)
        w_scale = tiles("w_scale", 2, [P, M], U8)
        xs_code = tiles("xs_code", 8, [P, 2 * P], U32)
        xs_scale = tiles("xs_scale", 8, [P, 2 * P], U8)
        yb = tiles("yb", 8, [P, M], F32)
        db_rows = tiles("db_rows", 2, [P, 4, M], BF16)
        db_mix = tiles("db_mix", 2, [P, M, 4], BF16)
        db_code = tiles("db_code", 2, [P, M], U32)
        db_scale = tiles("db_scale", 2, [P, M], U8)
        xa_rows = tile("xa_rows", [P, 4, 512], BF16)
        xa_mix = tiles("xa_mix", 2, [P, 2, 4, P, 4], BF16)
        xa_code = tiles("xa_code", 2, [P, D], U32)
        xa_scale = tiles("xa_scale", 2, [P, D], U8)
        u_big = tiles("u_big", 8, [P, M], BF16)
        coef = tiles("coef", 8, [P, M], F32)
        out_rows = coef
        step = tiles("step", 8, [P, M], F32)
        side = tiles("side", len(SIDE_TILES), [P, M], F32)
        row_sum = tile("row_sum", [P, 8], F32)
        side_sum = tile("side_sum", [P, len(SIDE_TILES)], F32)
        lam_sum = tile("lam_sum", [P, 2], F32)
        shift = tile("shift", [P, 1], F32)
        out_bf = tiles("out_bf", 8, [P, 2, P, 2], BF16)
        out_mix = tiles("out_mix", 2, [P, 512, 4], BF16)
        out_code = tiles("out_code", 2, [P, 512], U32)
        out_scale = tiles("out_scale", 2, [P, 512], U8)
        xs_mix, tanh_z, exp_lam, x_turned, bank = {}, {}, {}, {}, {}

        def columns(vec):
            return vec.rearrange("(g p t) -> p g t", g=2, t=4)

        nc.scalar.dma_start(out=s_bf[:], in_=columns(s))
        nc.gpsimd.dma_start(out=a_bf[:], in_=columns(a))
        nc.scalar.dma_start(out=b_bf[:], in_=columns(b))
        nc.vector.memset(zero[:], 0.0)
        nc.scalar.activation(out=zero[:], in_=zero[:], func=ACT.Tanh)

        x_hbm = x.rearrange("(g p t) d -> g t p d", g=2, t=4)
        w_hbm = w.rearrange("(g p t) m -> g p t m", g=2, t=4)
        y_hbm = y.rearrange("(g p t) m -> g p t m", g=2, t=4)
        lam_hbm = lam.rearrange("(g p t) m -> g p t m", g=2, t=4)

        def load_x(i):
            nc.sync.dma_start(out=x_in[i][:], in_=x_hbm[i // 4, i % 4])

        nc.sync.dma_start(out=w_in[0][:], in_=w_hbm[0])
        load_x(0)
        nc.sync.dma_start(out=w_in[1][:], in_=w_hbm[1])
        load_x(1)
        load_x(2)
        nc.sync.dma_start(out=y_in[0][:], in_=y_hbm[0])
        for i in range(3, 8):
            load_x(i)
        nc.sync.dma_start(out=y_in[1][:], in_=y_hbm[1])
        nc.sync.dma_start(out=lam_in[0][:], in_=lam_hbm[0])
        nc.sync.dma_start(out=lam_in[1][:], in_=lam_hbm[1])

        def flat(cols):
            return cols[:].rearrange("p g t -> p (g t)")

        make_identity(nc, ident[:])
        nc.gpsimd.tensor_copy(out=ident_bf[:], in_=ident[:])
        nc.gpsimd.memset(mean_weights[:], -1.0 / (D * M))
        nc.gpsimd.memset(ones_bf[:], 1.0)
        nc.gpsimd.memset(lam_sum[:, 1:2], float(D * M // P))
        nc.gpsimd.tensor_scalar(
            out=s_sign[:], in0=flat(s_bf), scalar1=TO_SIGN, scalar2=0.0, op0=ALU.mult, op1=ALU.add
        )
        nc.gpsimd.tensor_copy(out=a_col[:], in_=flat(a_bf))
        nc.gpsimd.tensor_copy(out=b_col[:], in_=flat(b_bf))
        nc.gpsimd.tensor_scalar(out=b_half[:], in0=flat(b_bf), scalar1=0.5, scalar2=0.0, op0=ALU.mult, op1=ALU.add)
        nc.gpsimd.tensor_scalar(
            out=b_neg_half[:], in0=flat(b_bf)[:, 0:1], scalar1=-0.5, scalar2=0.0, op0=ALU.mult, op1=ALU.add
        )

        def quantise(code, scale, mixed):
            nc.vector.quantize_mx(out=code.bitcast(FP8X4), scales=scale, in_=mixed)

        def interleave(dst, src):
            for copy, c in (
                (nc.vector.tensor_copy, slice(0, VECTOR_COLUMNS)),
                (nc.scalar.copy, slice(VECTOR_COLUMNS, M)),
            ):
                copy(
                    out=dst[:, c, :].rearrange("p (c i) t -> p c t i", i=4),
                    in_=src[:, :, c].rearrange("p t (c i) -> p c t i", i=4),
                )

        def quantise_w(g):
            quantise(w_code[g][:], w_scale[g][:], w_mix[g][:].rearrange("p m t -> p (m t)"))

        def turn_x(i):
            x_turned[i] = ps_x.tile([P, 2, 2, P], F32, name="x_turned")
            words = x_in[i][:].bitcast(F32)
            for g in range(2):
                for u in range(2):
                    nc.tensor.transpose(
                        x_turned[i][:, g, u, :], words[:, 256 * g + u : 256 * (g + 1) : 2], ident[:]
                    )

        def scale_x(i):
            xs_mix[i] = roll.tile([P, 2, P, 4], BF16, name="xs_mix", align_bytes=64)
            for g in range(2):
                factor = s_bf[:, g, :].unsqueeze(1).to_broadcast([P, P, 4])
                nc.vector.tensor_tensor(
                    out=xs_mix[i][:, g].rearrange("p n (u e) -> p n u e", e=2),
                    in0=x_turned[i][:, g].bitcast(BF16).rearrange("p u (n e) -> p n u e", e=2),
                    in1=factor.rearrange("p n (u e) -> p n u e", e=2),
                    op=ALU.mult,
                )

        def quantise_xs(i):
            quantise(xs_code[i][:], xs_scale[i][:], xs_mix[i][:].rearrange("p g n t -> p (g n t)"))

        def logits(i):
            z = ps_bank.tile([P, M], F32, name="bank")
            bank["z", i] = z
            for g in range(2):
                c = slice(P * g, P * g + P)
                nc.tensor.matmul_mx(
                    out=z[:],
                    lhsT=xs_code[i][:, c].bitcast(FP8X4),
                    lhsT_scale=xs_scale[i][:, c],
                    rhs=w_code[g][:].bitcast(FP8X4),
                    rhs_scale=w_scale[g][:],
                    start=(g == 0),
                    stop=(g == 1),
                )

        def tanh_half(i):
            tanh_z[i] = roll.tile([P, M], F32, name="tanh_z", align_bytes=64)
            nc.scalar.activation(out=tanh_z[i][:], in_=bank["z", i][:], func=ACT.Tanh, scale=0.5)

        def scale_y(i):
            source = y_in[i // 4][:, i % 4, :]
            if i == 0:
                nc.scalar.activation(
                    out=yb[i][:], in_=source, func=ACT.Identity, scale=b_col[:, 0:1], bias=b_neg_half[:]
                )
            else:
                nc.gpsimd.tensor_scalar(
                    out=yb[i][:], in0=source, scalar1=-0.5, scalar2=b_col[:, i : i + 1], op0=ALU.add, op1=ALU.mult
                )

        def residual(i):
            nc.vector.scalar_tensor_tensor(
                out=db_rows[i // 4][:, i % 4, :],
                in0=tanh_z[i][:],
                scalar=b_half[:, i : i + 1],
                in1=yb[i][:],
                op0=ALU.mult,
                op1=ALU.subtract,
            )

        def quantise_db(g):
            quantise(db_code[g][:], db_scale[g][:], db_mix[g][:].rearrange("p m t -> p (m t)"))

        def scale_xa_rows():
            for t in range(4):
                nc.vector.tensor_scalar(
                    out=xa_rows[:, t, :], in0=x_in[t][:, 0:512], scalar1=a_col[:, t : t + 1], scalar2=None, op0=ALU.mult
                )

        def interleave_xa_rows():
            source = xa_rows[:].rearrange("p t (q j) -> p j q t", j=4)
            nc.vector.tensor_copy(out=xa_mix[0][:, 0, 0:2], in_=source[:, 0:2])
            nc.scalar.copy(out=xa_mix[0][:, 0, 2:4], in_=source[:, 2:4])

        def diagonals(g):
            for i in range(4 * g, 4 * g + 4):
                nc.scalar.activation(out=diag_a[:, i, :], in_=ident_bf[:], func=ACT.Copy, scale=a_col[:, i : i + 1])

        def make_xa(g, chunk):
            product = ps_bank.tile([P, 4, P], F32, name="bank")
            for t in range(4):
                nc.tensor.matmul(
                    out=product[:, t, :],
                    lhsT=diag_a[:, 4 * g + t, :],
                    rhs=x_in[4 * g + t][:, P * chunk : P * chunk + P],
                    start=True,
                    stop=True,
                )
            q0 = 32 * (chunk % 4)
            nc.scalar.copy(
                out=xa_mix[g][:, chunk // 4, :, q0 : q0 + 32, :],
                in_=product[:].rearrange("p t (q j) -> p j q t", j=4),
            )

        def quantise_xa(g, half):
            c = slice(512 * half, 512 * half + 512)
            quantise(xa_code[g][:, c], xa_scale[g][:, c], xa_mix[g][:, half].rearrange("p j q t -> p (j q t)"))

        def enlarge_u(i):
            nc.vector.tensor_scalar(
                out=u_big[i][:],
                in0=w_in[i // 4][:, i % 4, :],
                scalar1=s_sign[:, i : i + 1],
                scalar2=1.0,
                op0=ALU.mult,
                op1=ALU.min,
            )

        def exponential(i):
            exp_lam[i] = roll.tile([P, M], F32, name="exp_lam", align_bytes=64)
            nc.scalar.activation(out=exp_lam[i][:], in_=lam_in[i // 4][:, i % 4, :], func=ACT.Exp, bias=zero[:])

        def coefficient(i):
            nc.vector.scalar_tensor_tensor(
                out=coef[i][:], in0=u_big[i][:], scalar=-1.0, in1=exp_lam[i][:], op0=ALU.max, op1=ALU.mult
            )

        def gradient(i):
            grad = ps_bank.tile([P, M], F32, name="bank")
            bank["grad", i] = grad
            c = slice(P * i, P * i + P)
            for g in range(2):
                nc.tensor.matmul_mx(
                    out=grad[:],
                    lhsT=xa_code[g][:, c].bitcast(FP8X4),
                    lhsT_scale=xa_scale[g][:, c],
                    rhs=db_code[g][:].bitcast(FP8X4),
                    rhs_scale=db_scale[g][:],
                    start=(g == 0),
                    stop=(g == 1),
                )

        def make_step(i):
            nc.vector.scalar_tensor_tensor(
                out=step[i][:],
                in0=bank["grad", i][:],
                scalar=STEP,
                in1=coef[i][:],
                op0=ALU.mult,
                op1=ALU.mult,
                accum_out=row_sum[:, i : i + 1],
            )

        chunks = [(0, k) for k in range(4, 8)] + [(1, k) for k in range(8)]
        todo = [lambda: scale_y(0)]
        for k in range(7):
            todo += [lambda k=k: scale_y(k + 1), lambda k=k: make_xa(*chunks[k])]
        for k in range(5):
            todo += [lambda k=k: exponential(k), lambda k=k: make_xa(*chunks[7 + k])]
        todo += [lambda k=k: exponential(k) for k in range(5, 8)]

        def take(count):
            for item in todo[:count]:
                item()
            for item in todo[:count]:
                todo.remove(item)

        turn_x(0)
        turn_x(1)
        interleave(w_mix[0], w_in[0])
        quantise_w(0)
        scale_x(0)
        interleave(w_mix[1], w_in[1])
        quantise_xs(0)
        scale_x(1)
        quantise_w(1)
        diagonals(0)
        take(1)
        diagonals(1)
        quantise_xs(1)
        turn_x(2)
        for i in range(1, 11):
            if i <= 8:
                logits(i - 1)
            if 2 <= i < 8:
                scale_x(i)
                if i < 7:
                    turn_x(i + 1)
            if i <= 8:
                tanh_half(i - 1)
            if i >= 3:
                residual(i - 3)
            if 2 <= i < 8:
                quantise_xs(i)
            if i <= 9:
                take(2)
            if i == 1:
                for k in range(4):
                    enlarge_u(k)
            if i == 3:
                scale_xa_rows()
            if i == 4:
                interleave_xa_rows()
            if i == 6:
                interleave(db_mix[0], db_rows[0])
            if i == 7:
                for k in range(4, 8):
                    enlarge_u(k)
            if i == 8:
                quantise_xa(0, 0)
            if i == 9:
                quantise_db(0)

        quantise_xa(0, 1)
        coefficient(0)
        interleave(db_mix[1], db_rows[1])
        take(len(todo))
        coefficient(1)
        quantise_db(1)
        coefficient(2)
        quantise_xa(1, 0)
        coefficient(3)

        sums = ps_sum.tile([P, 2], F32, name="sums")
        for k in range(32):
            nc.tensor.matmul(
                out=sums[:, 0:1],
                lhsT=lam_in[k // 16][:, (k // 4) % 4, P * (k % 4) : P * (k % 4) + P],
                rhs=ones_bf[:],
                start=(k == 0),
                stop=(k == 31),
            )
        coefficient(4)
        quantise_xa(1, 1)
        nc.vector.tensor_copy(out=lam_sum[:, 0:1], in_=sums[:, 0:1])
        for i in range(4):
            gradient(i)
        for i in range(5, 8):
            coefficient(i)
        for i in SIDE_TILES:
            nc.scalar.activation(out=side[i][:], in_=bank["grad", i][:], func=ACT.Copy, scale=STEP)
        for i in SIDE_TILES:
            nc.gpsimd.tensor_tensor(out=step[i][:], in0=side[i][:], in1=coef[i][:], op=ALU.mult)
            nc.scalar.activation(out=side[i][:], in_=step[i][:], func=ACT.Identity, accum_out=side_sum[:, i : i + 1])
        for i in range(len(SIDE_TILES), 8):
            make_step(i)
            if i + 2 < 8:
                gradient(i + 2)
            if i in (EARLY_GPSIMD, EARLY_VECTOR):
                engine = nc.gpsimd if i == EARLY_GPSIMD else nc.vector
                engine.tensor_tensor(out=step[i][:], in0=step[i][:], in1=lam_in[i // 4][:, i % 4, :], op=ALU.add)

        parts = [lam_sum[:, 1:2], lam_sum[:, 0:1]]
        for i in (2, 3, 0, 4, 5, 1, 6, 7):
            parts.append((side_sum if i in SIDE_TILES else row_sum)[:, i : i + 1])
        for k, part in enumerate(parts):
            nc.tensor.matmul(
                out=sums[:, 1:2], lhsT=mean_weights[:], rhs=part, start=(k == 0), stop=(k == len(parts) - 1)
            )
        nc.vector.tensor_copy(out=shift[:], in_=sums[:, 1:2])

        out_hbm = out_0.rearrange("(g p t) m -> g t p m", g=2, t=4)
        code_hbm = out_1.rearrange("g p m t -> (g p) (m t)").bitcast(I32)
        scale_hbm = out_2.rearrange("g q m -> (g q) m").bitcast(I32)

        def result(i):
            if i in (EARLY_GPSIMD, EARLY_VECTOR):
                nc.scalar.activation(out=out_rows[i][:], in_=step[i][:], func=ACT.Identity, bias=shift[:])
            else:
                nc.vector.scalar_tensor_tensor(
                    out=out_rows[i][:],
                    in0=step[i][:],
                    scalar=sums[:, 1:2],
                    in1=lam_in[i // 4][:, i % 4, :],
                    op0=ALU.add,
                    op1=ALU.add,
                )
            nc.sync.dma_start(out=out_hbm[i // 4, i % 4], in_=out_rows[i][:])

        def word_order(rows):
            return rows[:].rearrange("p (q u e) -> p u q e", u=2, e=2)

        def round_early(i):
            nc.vector.tensor_scalar(
                out=out_bf[i][:], in0=word_order(step[i]), scalar1=shift[:], scalar2=None, op0=ALU.add
            )

        def round_rows(i, copy):
            copy(out=out_bf[i][:], in_=word_order(out_rows[i]))

        turned = {}

        def turn_result(*which):
            for i in which:
                if i // 2 not in turned:
                    pair = ps_bank.tile([P, 2, 2, P], F32, name="bank")
                    turned[i // 2] = pair
                words = out_bf[i][:].rearrange("p u q e -> p (u q e)").bitcast(F32)
                for u in range(2):
                    nc.tensor.transpose(turned[i // 2][:, i % 2, u, :], words[:, P * u : P * u + P], ident[:])

        def place_pair(k, copy):
            words = out_mix[k // 2][:].rearrange("p m t -> p (m t)").bitcast(F32)
            t0 = 2 * (k % 2)
            copy(
                out=words.rearrange("p (q t u) -> p q t u", t=4, u=2)[:, :, t0 : t0 + 2, :],
                in_=turned[k][:].rearrange("p t u q -> p q t u"),
            )

        def quantise_result(g):
            quantise(out_code[g][:], out_scale[g][:], out_mix[g][:].rearrange("p m t -> p (m t)"))
            nc.sync.dma_start(out=code_hbm[:, 512 * g : 512 * g + 512], in_=out_code[g][:].bitcast(I32))

        def store_scales(g):
            for q in range(4):
                nc.scalar.dma_start(
                    out=scale_hbm[4 * q : 4 * q + 4, P * g : P * g + P],
                    in_=out_scale[g][32 * q : 32 * q + 4, :].bitcast(I32),
                )

        by_vector, by_scalar = nc.vector.tensor_copy, nc.scalar.copy
        result(0)
        result(2)
        round_early(2)
        round_rows(0, by_scalar)
        result(1)
        result(3)
        round_rows(1, by_scalar)
        result(7)
        round_early(7)
        result(4)
        turn_result(0, 1)
        round_rows(3, by_vector)
        place_pair(0, by_scalar)
        result(5)
        round_rows(4, by_scalar)
        turn_result(2, 3)
        turn_result(7)
        round_rows(5, by_vector)
        place_pair(1, by_scalar)
        result(6)
        turn_result(4, 5)
        round_rows(6, by_vector)
        place_pair(2, by_scalar)
        quantise_result(0)
        turn_result(6)
        store_scales(0)
        place_pair(3, by_vector)
        quantise_result(1)
        store_scales(1)
